import numpy as np, ml_dtypes
CORES = [16,17,18,19,32,33,34,35]
N = 8
BF = ml_dtypes.bfloat16
def gentries(a):
    return np.ascontiguousarray(a.reshape(8, 16, -1).transpose(0, 2, 1)).reshape(8, -1)
def gtable(e):
    e = np.asarray(e); return np.ascontiguousarray(e.reshape(8, -1, 16).transpose(0, 2, 1)).reshape(128, -1).astype(np.int32)
P, L, G, RO, J = 2048, 2, 2048, 3, 1
K = L * G; W = P + K
H = P // 16; C = G // 32
B = 2 ** J + 2; Y = 16; T = 3 + B + 2 * Y
ENDS = [RO - 1, 2 * RO - 2, 2 * RO - 1, 2 * RO - 1 + B, 2 * RO - 1 + 2 * B, 2 * RO - 1 + 2 * B + 2 * Y, 2 * RO + 1 + 2 * B + 3 * Y]; X = ENDS[-1] + 1
TIES = [[28, 17, 21, 9], [41, 18, 23, 5], [42, 38, 35, 13], [44, 27, 18, 7], [45, 22, 34, 4], [45, 35, 43, 14], [49, 48, 43, 15], [52, 5, 50, 11]]
def pick(rng, top, shape, pw):
    return np.minimum((top * rng.random(shape) ** pw).astype(np.int64), top - 1)
def wiring(rng, kinds=(0, 1, 2, 3, 4, 5, 6), pw=(1.0,) * 8):
    o = np.argsort(rng.random((8, P)), axis=1); z = o[:, :16]; q = o[:, 16:16 + 8 * H].reshape(8, 4, H, 2); ex = o[:, 16 + 8 * H:16 + 8 * H + X]; k = np.arange(K)
    fa = np.zeros((N, 8, K), np.int64); fb = np.zeros((N, 8, K), np.int64); cd = np.zeros((8, K), np.int64); tp = np.zeros((8, P), np.int64)
    for g in range(8):
        w = pw[g]; tops = P + k // G * G; pairs = []
        last = np.sort(np.append(G - 512 + rng.permutation(511)[:T - 1], G - 1)); sp = (L - 1) * G + last
        fa[:, g] = pick(rng, tops, (N, K), w); fb[:, g] = pick(rng, tops, (N, K), w); cd[g] = pick(rng, P + k, K, w); tp[g] = pick(rng, W, P, w)
        for l in range(L):
            top = P + l * G; m = l * G + rng.permutation(G)
            if l == L - 1: m = l * G + np.concatenate([rng.permutation(np.setdiff1d(np.arange(G), last)), last])
            pr = np.sort(m[:14 * C].reshape(7, C, 2), axis=2)
            for j, kind in enumerate(kinds):
                n1, n2 = pr[j, :, 0], pr[j, :, 1]
                a1 = pick(rng, top, (N, C), w); b1 = pick(rng, top, (N, C), w); a2 = a1.copy(); i = rng.integers(0, H, (N, C))
                if kind == 3: i = np.tile(i[:1], (N, 1)); b1 = np.tile(z[g, rng.integers(0, 16, C)], (N, 1))
                if kind >= 2: s = q[g, (0, 1, 2, 2, 3)[kind - 2]]; a1, a2 = s[i, 0], s[i, 1]
                if kind in (1, 5): a2[rng.integers(0, N, C), np.arange(C)] = pick(rng, top, C, w)
                if kind in (2, 4, 6) and rng.random() < 0.5: fa[:, g, n1] = b1; fb[:, g, n1] = a1; fa[:, g, n2] = b1; fb[:, g, n2] = a2
                else: fa[:, g, n1] = a1; fb[:, g, n1] = b1; fa[:, g, n2] = a2; fb[:, g, n2] = b1
                cd[g, n2] = P + n1
                if kind == 4: pairs.append(pr[j])
            s = m[14 * C:18 * C]; a1 = pick(rng, top, 4 * C, w)
            fa[:, g, s] = a1; fb[:, g, s] = z[g, rng.integers(0, 16, 4 * C)]; cd[g, s] = a1
            if l > 0:
                s = m[18 * C:22 * C]; i = pick(rng, l * G, 4 * C, w)
                fa[:, g, s] = fa[:, g, i]; fb[:, g, s] = fb[:, g, i]; cd[g, s] = P + i
            s = np.sort(m[22 * C:28 * C].reshape(C, 6), axis=1)
            fa[:, g, s] = pick(rng, top, (N, C, 1), w); fb[:, g, s] = pick(rng, top, (N, C, 1), w); cd[g, s[:, 1:]] = P + s[:, :-1]
        pt = np.concatenate(pairs)
        tp[g, z[g, :4]] = z[g, :4]; tp[g, q[g, 2, :, 1]] = tp[g, q[g, 2, :, 0]]; tp[g, q[g, 3]] = P + pt[rng.integers(0, len(pt), H)]
        ua, ub, us, e, h, nr, vw, full = np.split(ex[g], ENDS); t = rng.permutation(T - 1)
        n0 = np.sort(sp[t[:2]]); n1 = np.sort(sp[t[2:2 + B]]); n2 = np.sort(sp[t[2 + B:]].reshape(Y, 2), axis=1)
        fb[:, g, sp] = z[g, rng.integers(0, 4, (N, T))]
        fa[:, g, n0] = ua[0]; fa[:, g, K - 1] = ub[0]; cd[g, n0[1]] = P + n0[0]; cd[g, K - 1] = P + n0[1]
        fa[:, g, n1] = e; cd[g, n1[1:]] = P + n1[:-1]
        fa[:, g, n2] = nr.reshape(Y, 2); cd[g, n2[:, 1]] = P + n2[:, 0]
        tp[g, ua] = np.append(ua[1:], us); tp[g, ub] = np.append(ub[1:], us); tp[g, us] = us; tp[g, e] = h; tp[g, h] = e; tp[g, nr] = nr; tp[g, full] = full
        tp[g, vw] = P + np.concatenate([[K - 1, n1[-1]], n2[:, 1]])
    return z, q, ex, fa, fb, cd, tp
def gaps(rng):
    S = 16 * N; a = 16 * rng.integers(0, N, 3) + rng.integers(0, 14, 3); b = 16 * rng.integers(0, N - 2, 3) + rng.integers(0, 16, 3); u = 2 * rng.integers(0, 8 * N, 2)
    c = [([S - 1], [1]), ([0], [1]), ([S - 16], [1]), ([a[0], a[0] + 1], [2, -1]), ([a[1], a[1] + 1], [-1, 2]), ([b[0], b[0] + 16], [2, -1]), ([b[1], b[1] + 16], [-1, 2]),
         ([u[0], u[0] + 1], [255, -1]), ([u[1], u[1] + 1], [-1, 255]), ([a[2], a[2] + 1, a[2] + 2], [1, -2, 1]), ([b[2], b[2] + 16, b[2] + 32], [1, -2, 1])]
    for i in rng.integers(0, len(TIES), 2): c.append((TIES[i], [1, 1, -1, -1]))
    for i in range(3): c.append((rng.permutation(S)[:4], [1, 1, -1, -1]))
    return c
def plant(rng, xx, z, q, ex, lo=(0,) * 8, hi=(16 * N,) * 8):
    for g in range(8):
        v = xx[g]; n0, n1 = q[g, 1, :, 0], q[g, 1, :, 1]; s = hi[g] - lo[g]
        v[:, z[g]] = 0; v[:, q[g, 0, :, 1]] = v[:, q[g, 0, :, 0]]
        v[:, n0] = np.clip(v[:, n0], 1, 254); v[:, n1] = v[:, n0]
        i = rng.integers(0, s, H); j = (i + 1 + rng.integers(0, s - 1, H)) % s; mode = rng.permutation(np.arange(H) % 4)
        v[lo[g] + i, n1] += np.where(mode < 2, 1, np.where(mode == 2, -1, 0)); v[lo[g] + j, n1] -= (mode == 1).astype(np.int64)
        ua, ub, us, e, h, nr, vw, full = np.split(ex[g], ENDS)
        i = rng.integers(0, 16 * N, RO - 1); v[i, ub] = 255 - v[i, ua]
        v[rng.integers(0, 16 * N), e] = 255 * (np.arange(B) % 2); v[:, h] = v[:, h[:1]]; v[:, full] = 255
        for j, (places, d) in enumerate(gaps(rng)):
            places = np.array(places); d = np.array(d); n = nr[2 * j:2 * j + 2]
            if rng.random() < 0.5: n = n[::-1]
            c = np.clip(v[:, n[0]], 2, 253); c[places] = np.where(d == 255, 0, c[places]); v[:, n[0]] = c
            c = c.copy(); c[places] += d; v[:, n[1]] = c
    return xx
def quiet(g, xx, z, ex, fa, fb, cd):
    v = np.zeros((N, 16, W), np.int64); v[..., :P] = xx[g].reshape(N, 16, P)
    for l in range(L):
        s = slice(l * G, (l + 1) * G)
        v[..., P + l * G:P + (l + 1) * G] = np.minimum(np.take_along_axis(v, fa[:, g, None, s], 2), 255 - np.take_along_axis(v, fb[:, g, None, s], 2))
    own = v[..., P:]; same = np.all(own == v[..., cd[g]], axis=(0, 1)); zero = np.all(own == 0, axis=(0, 1))
    cd[g] = np.where(same, np.where(zero, ex[g, -1], z[g, 0]), cd[g])
def pack(xx, fa, fb, cd, tp):
    x = np.ascontiguousarray(xx.reshape(8, N, 16, P).transpose(1, 0, 2, 3)).reshape(N, 128, P)
    return {"x": x.astype(np.float32).astype(BF), "fa": np.stack([gtable(e) for e in fa]), "fb": np.stack([gtable(e) for e in fb]), "cd": np.stack([gtable(cd)] * N), "tp": np.stack([gtable(tp)] * N)}
def setup_inputs(rng):
    z, q, ex, fa, fb, cd, tp = wiring(rng)
    return pack(plant(rng, rng.integers(0, 256, (8, 16 * N, P)), z, q, ex), fa, fb, cd, tp)
def setup_inputs_near(rng):
    z, q, ex, fa, fb, cd, tp = wiring(rng, kinds=(3, 3, 3, 3, 4, 5, 1))
    for g in range(8): tp[g, z[g]] = z[g]; tp[g, q[g, 1, :H // 2]] = q[g, 1, :H // 2]
    one = (0, N - 1, 1, N - 2); lo = [16 * one[g] if g < 4 else 0 for g in range(8)]; hi = [16 * one[g] + 16 if g < 4 else 16 * N for g in range(8)]
    xx = plant(rng, rng.integers(0, 256, (8, 16 * N, P)), z, q, ex, lo, hi)
    for g in (4, 7): quiet(g, xx, z, ex, fa, fb, cd)
    return pack(xx, fa, fb, cd, tp)
def setup_inputs_chains(rng):
    z, q, ex, fa, fb, cd, tp = wiring(rng); n = G // 32; h = n // 2
    for g in range(1, 8, 2):
        last = None
        for l in range(L):
            top = P + l * G; s = l * G + np.sort(rng.permutation(G).reshape(n, 32), axis=1)
            a = rng.integers(0, top, (N, n)); b = rng.integers(0, top, (N, n))
            if l > 0: a[:, :h] = P + last[:h]; b[:, :h] = z[g, 0]; cd[g, s[:h, 0]] = P + last[:h]
            fa[:, g, s] = a[:, :, None]; fb[:, g, s] = b[:, :, None]; cd[g, s[:, 1:]] = P + s[:, :-1]
            cut = rng.random((n, 32)) < 0.08; cut[:, 0] = False; cut[0, 16] = True; c = s[cut]
            fa[rng.integers(0, N, len(c)), g, c] = rng.integers(0, top, len(c)); last = s[:, -1]
    return pack(plant(rng, rng.integers(0, 256, (8, 16 * N, P)), z, q, ex), fa, fb, cd, tp)
def setup_inputs_flat(rng):
    z, q, ex, fa, fb, cd, tp = wiring(rng)
    xx = plant(rng, 255 * rng.integers(0, 2, (8, 16 * N, P)), z, q, ex); o = rng.permutation(8)
    xx[o[0]] = 0; xx[o[1]] = 255
    return pack(xx, fa, fb, cd, tp)
def setup_inputs_ends(rng):
    z, q, ex, fa, fb, cd, tp = wiring(rng); k = np.arange(K); tops = P + k // G * G
    fa[:, 0] = np.where(rng.random((N, K)) < 0.5, 0, tops - 1); fb[:, 0] = np.where(rng.random((N, K)) < 0.5, 0, tops - 1)
    fb[:, 1] = fa[:, 1]
    cd[2] = P + k - 1
    m = rng.random(K) < 0.5; fa[:, 3, m] = 0; fb[:, 3, m] = z[3, 0]; cd[3] = 0
    tp[4] = rng.choice(np.array([0, P - 1, P, W - 1]), P)
    cd[5] = np.where(rng.random(K) < 0.5, 0, P + k - 1); fa[:, 5] = np.where(rng.random(K) < 0.5, tops - 1, fa[:, 5])
    fa[:, 6] = tops - 1; fb[:, 6] = z[6, 0]; cd[6] = P + k - 1
    return pack(plant(rng, rng.integers(0, 256, (8, 16 * N, P)), z, q, ex), fa, fb, cd, tp)
def setup_inputs_spread(rng):
    pw = rng.permutation(np.array([0.35, 0.35, 0.6, 1.0, 1.0, 1.5, 3.0, 3.0])); z, q, ex, fa, fb, cd, tp = wiring(rng, pw=pw)
    e = np.exp2(rng.integers(-3, 4, (8, 1, P)) + rng.integers(-1, 2, (8, 16 * N, 1)))
    return pack(plant(rng, np.minimum((256 * rng.random((8, 16 * N, P)) ** e).astype(np.int64), 255), z, q, ex), fa, fb, cd, tp)
def check_inputs(d):
    bad = []; k = np.arange(K); x = np.asarray(d["x"]).astype(np.float32)
    if not (np.all(x >= 0) and np.all(x <= 255) and np.all(x == np.floor(x))): bad.append("whole numbers from 0 to 255 in x")
    for name, top in (("fa", P + k // G * G), ("fb", P + k // G * G), ("cd", P + k), ("tp", W)):
        e = np.stack([gentries(s) for s in d[name]]).astype(np.int64)
        if np.any(e < 0) or np.any(e >= top): bad.append("range of " + name)
    for name in ("cd", "tp"):
        if np.any(d[name] != d[name][:1]): bad.append(name + " alike on all ranks")
    return bad
def reference(x, fa, fb, cd, tp):
    now = x.astype(np.float32).astype(np.int32).reshape(N, 8, 16, P)
    a = np.stack([gentries(e) for e in fa]).astype(np.int64); b = np.stack([gentries(e) for e in fb]).astype(np.int64)
    c = gentries(cd[0]).astype(np.int64); taps = gentries(tp[0]).astype(np.int64)
    for rnd in range(RO):
        v = np.zeros((N, 8, 16, W), np.int32); v[..., :P] = now
        for l in range(L):
            s = slice(l * G, (l + 1) * G)
            v[..., P + l * G:P + (l + 1) * G] = np.minimum(np.take_along_axis(v, a[:, :, None, s], 3), 255 - np.take_along_axis(v, b[:, :, None, s], 3))
        differ = v[..., P:] != np.take_along_axis(v, c[None, :, None, :], 3)
        mm = np.add.reduce(np.add.reduce(differ.astype(np.int32), axis=2), axis=0)
        rep = np.tile(np.arange(W), (8, 1)); rep[:, P:] = np.where(mm == 0, c, rep[:, P:])
        for j in range(J): rep = np.take_along_axis(rep, rep, 1)
        a = np.take_along_axis(rep[None], a, 2); b = np.take_along_axis(rep[None], b, 2)
        taps = np.take_along_axis(rep, taps, 1)
        now = np.take_along_axis(v, taps[None, :, None, :], 3)
    return {"yv": v.reshape(N, 128, W).astype(np.float32).astype(BF), "ya": np.stack([gtable(e) for e in a]).astype(np.float32), "yb": np.stack([gtable(e) for e in b]).astype(np.float32),
            "yt": np.stack([gtable(taps)] * N).astype(np.float32)}

@@ -1,0 +1,513 @@
+from concourse.bass import DstId, RemoteDMATransfer
+from concourse.mybir import AluOpType, ActivationFunctionType
+
+SHARE = 68
+SHARE2 = 72
+LAST = 16
+LOOK1 = 2
+LOOK2 = 3
+STAGE2 = True
+BIG = 8192
+CUTS = [0, 26, 52, 78, 104, 128]
+
+SCRATCH = {
+    "v1": ("sbuf", [128, 8192], "bfloat16"),
+    "v2": ("sbuf", [128, 8192], "bfloat16"),
+    "v3": ("sbuf", [128, 8192], "bfloat16"),
+    "win": ("sbuf", [128, 4112], "bfloat16"),
+    "tw": ("sbuf", [128, 2048], "bfloat16"),
+    "ad": ("sbuf", [128, 1024], "bfloat16"),
+    "ab": ("sbuf", [128, 512], "int32"),
+    "abu": ("sbuf", [128, 512], "uint16"),
+    "abf": ("sbuf", [128, 512], "float32"),
+    "aby": ("sbuf", [128, 256], "int32"),
+    "abx": ("sbuf", [128, 256], "uint16"),
+    "abz": ("sbuf", [128, 256], "uint16"),
+    "w1": ("sbuf", [128, 256], "int32"),
+    "w2": ("sbuf", [128, 256], "float32"),
+    "w3": ("sbuf", [128, 256], "float32"),
+    "cdi": ("sbuf", [128, 256], "int32"),
+    "cdu": ("sbuf", [128, 256], "uint16"),
+    "cdf": ("sbuf", [128, 256], "float32"),
+    "tpi": ("sbuf", [128, 128], "int32"),
+    "lst": ("sbuf", [128, 512], "uint16"),
+    "own": ("sbuf", [128, 32], "int32"),
+    "chl": ("sbuf", [128, 64], "bfloat16"),
+    "ww": ("sbuf", [128, 576], "bfloat16"),
+    "wp": ("sbuf", [128, 160], "bfloat16"),
+    "bnd": ("sbuf", [128, 48], "bfloat16"),
+    "sel": ("sbuf", [128, 16], "float32"),
+    "ti": ("sbuf", [128, 16], "float32"),
+    "pi": ("sbuf", [128, 4], "int32"),
+    "pj": ("sbuf", [128, 4], "int32"),
+    "pk": ("sbuf", [128, 4], "float32"),
+    "stt": ("sbuf", [128, 256], "float32"),
+    "off": ("sbuf", [128, 192], "uint16"),
+    "sm": ("sbuf", [128, 48], "float32"),
+    "gp": ("sbuf", [128, 256], "bfloat16"),
+    "cnt": ("sbuf", [128, 768], "bfloat16"),
+    "su": ("sbuf", [128, 48], "uint16"),
+    "sb": ("sbuf", [128, 32], "bfloat16"),
+    "ctab": ("dram", [2, 128, 32], "bfloat16"),
+    "lb0": ("dram", [8, 128, 16], "uint16"),
+    "lb1": ("dram", [8, 128, 16], "uint16"),
+    "lb2": ("dram", [8, 128, 16], "uint16"),
+    "lb3": ("dram", [8, 128, 32], "bfloat16"),
+    "lb4": ("dram", [8, 128, 16], "float32"),
+    "pp": ("psum", [128, 512], "float32"),
+    "pv": ("psum", [128, 512], "float32"),
+}
+for _k in range(2):
+    for _n in ("tb", "vc"):
+        SCRATCH["%s%d" % (_n, _k)] = ("sbuf", [128, 2048], "bfloat16")
+    SCRATCH["gq%d" % _k] = ("sbuf", [128, 512], "bfloat16")
+    SCRATCH["px%d" % _k] = ("psum", [128, 512], "float32")
+for _k in range(4):
+    SCRATCH["pd%d" % _k] = ("psum", [128, 512], "float32")
+for _k in range(6):
+    SCRATCH["la%d" % _k] = ("dram", [8, 128, 16], "bfloat16")
+    SCRATCH["sg%d" % _k] = ("dram", [8, 128, 16], "bfloat16")
+
+SEMAPHORES = (["cv", "cs", "ct", "cg", "loc"] + ["aa%d" % k for k in range(6)] + ["ab%d" % k for k in range(5)]
+              + ["d%d" % k for k in range(48)])
+SIZE = {"bfloat16": 2, "uint16": 2, "float32": 4, "int32": 4}
+A = AluOpType
+F = ActivationFunctionType
+WC, WF, WM, WE = 0, 144, 288, 432
+
+
+def deal_engines(src, cores, topo):
+    far = [c for c in cores if topo.chip(c) != topo.chip(src)]
+    near = [c for c in cores if c != src and topo.chip(c) == topo.chip(src)]
+    out = {}
+    used = []
+    for group in (far, near):
+        if not group:
+            continue
+        pool = [e for e in topo.engines(src, group[0]) if e not in used]
+        for n, c in enumerate(group):
+            left = len(group) - n
+            k = 1
+            while 2 * k + (left - 1) * k <= len(pool):
+                k *= 2
+            out[c] = pool[:k]
+            used += pool[:k]
+            pool = pool[k:]
+    return out
+
+
+def rank_program(g, core, T, topo):
+    r = T.rank_of(core)
+    if r is None:
+        return
+    cores = list(T.cores)
+    Q = {"g": g, "v": g.vector, "s": g.scalar, "t": g.tensor, "y": g.sync}
+    V, S, PE = g.vector, g.scalar, g.tensor
+    known = {q: {} for q in Q}
+    total = {}
+    recs = []
+    ndma = [0]
+
+    def span(reg):
+        name, c0, c1 = reg
+        where, shape, dtp = SCRATCH[name]
+        if where != "sbuf":
+            return (name, 0, 1 << 30)
+        z = SIZE[dtp]
+        return (name, c0 * z // 16 * 16, (c1 * z + 15) // 16 * 16)
+
+    def op(q, fn, reads, writes, dma=False):
+        rd = [span(x) for x in reads]
+        wr = [span(x) for x in writes]
+        needs = {}
+        for (q2, rd2, wr2, s2, v2, clock) in recs:
+            hit = False
+            for (n, a, b) in rd + wr:
+                ps = SCRATCH[n][0] == "psum"
+                if ps and q2 == q:
+                    continue
+                for (n2, a2, b2) in wr2 + (rd2 if (ps or (n, a, b) in wr) else []):
+                    if n2 == n and a < b2 and a2 < b:
+                        hit = True
+            if hit and needs.get(s2, (0, None))[0] < v2:
+                needs[s2] = (v2, clock)
+        for s2 in needs:
+            v2 = needs[s2][0]
+            if known[q].get(s2, 0) >= v2:
+                continue
+            if any(s3 != s2 and needs[s3][1].get(s2, 0) >= v2 for s3 in needs):
+                continue
+            Q[q].wait_ge(T.sem[s2], v2)
+        for s2 in needs:
+            for s3, v3 in needs[s2][1].items():
+                if known[q].get(s3, 0) < v3:
+                    known[q][s3] = v3
+        res = fn()
+        if res is None:
+            return
+        if dma:
+            sem = "d%d" % ndma[0]
+            ndma[0] += 1
+            val = 16 * len(res)
+            for ins in res:
+                ins.then_inc(T.sem[sem], 16)
+        else:
+            sem = "c" + q
+            val = total.get(sem, 0) + 1
+            res.then_inc(T.sem[sem], 1)
+        total[sem] = val
+        clock = dict(known[q])
+        clock[sem] = val
+        recs.append((q, rd, wr, sem, val, clock))
+
+    def dma(q, pairs, reads, writes):
+        op(q, lambda: [Q[q].dma_start(o, i) for (o, i) in pairs], reads, writes, True)
+
+    plans = {c: deal_engines(c, cores, topo) for c in cores}
+    arrive = sum(len(plans[c][core]) for c in cores if c != core)
+
+    def exchange(pairs, reg, source, src_of, land, sem):
+        dma("y", pairs, [reg], [(land, 0, 1)] + ([source] if source != reg else []))
+        def send():
+            trs = []
+            for k, c in enumerate(cores):
+                if c == core:
+                    continue
+                rid, pid, _ = topo.addr(c)
+                trs.append(RemoteDMATransfer(dst_ids=[DstId(rid=rid, pnc=pid)],
+                                             dma_engine_mask=sum(1 << e for e in plans[core][c]),
+                                             remote_sem=T.sem[sem], src=src_of(k), dst=T[land][r]))
+            g.remote_dma_fused(trs, local_sem=T.sem.loc)
+            total["loc"] = total.get("loc", 0) + sum(len(plans[core][c]) for c in plans[core])
+        op("g", send, [source], [])
+        total[sem] = arrive
+        recs.append(("far", [], [span((land, 0, 1))], sem, arrive, {sem: arrive}))
+
+    def spread(src, reg, land, sem):
+        if STAGE2:
+            exchange([(T[land][r], src)], reg, (land, 0, 1), lambda k: T[land][r], land, sem)
+        else:
+            exchange([(T[land][r], src)], reg, reg, lambda k: src, land, sem)
+
+    def vts(dst, d0, d1, src, s0, s1, *ops):
+        a = (ops[1], None, ops[0]) if len(ops) == 2 else (ops[1], ops[3], ops[0], ops[2])
+        op("v", lambda: V.tensor_scalar(T[dst][:, d0:d1], T[src][:, s0:s1], *a), [(src, s0, s1)], [(dst, d0, d1)])
+
+    def vtt(dst, d0, n, a, a0, b, b0, o):
+        op("v", lambda: V.tensor_tensor(T[dst][:, d0:d0 + n], T[a][:, a0:a0 + n], T[b][:, b0:b0 + n], o),
+           [(a, a0, a0 + n), (b, b0, b0 + n)], [(dst, d0, d0 + n)])
+
+    def vcp(dst, d0, src, s0, n, step=1):
+        d1 = d0 + step * (n - 1) + 1
+        op("v", lambda: V.tensor_copy(T[dst][:, d0:d1:step], T[src][:, s0:s0 + n]), [(src, s0, s0 + n)], [(dst, d0, d1)])
+
+    def fill(dst, d0, d1, value):
+        op("v", lambda: V.memset(T[dst][:, d0:d1], value), [], [(dst, d0, d1)])
+
+    def gather(q, dst, d0, win, w0, w1, ofs, o0, o1, minus=None, other=None, how=A.min):
+        n = 16 * (o1 - o0)
+        src = T[win][:, w0:w1].indirect(T[ofs][:, o0:o1])
+        out = T[dst][:, d0:d0 + n]
+        reads = [(win, w0, w1), (ofs, o0, o1)]
+        if other:
+            reads.append((other[0], other[1], other[1] + n))
+            fn = lambda: V.tensor_tensor(out, src, T[other[0]][:, other[1]:other[1] + n], how)
+        elif minus is not None and q == "v":
+            fn = lambda: V.tensor_scalar(out, src, -1.0, minus, A.mult, A.add)
+        elif minus is not None:
+            fn = lambda: S.activation(out, src, F.Identity, bias=minus, scale=-1.0)
+        elif q == "v":
+            fn = lambda: V.tensor_copy(out, src)
+        else:
+            fn = lambda: S.activation(out, src, F.Copy)
+        op(q, fn, reads, [(dst, d0, d0 + n)])
+
+    def shared(dst, d0, win, w0, w1, c, n):
+        gather("s", dst, d0, win, w0, w1, "lst", c, c + n)
+        gather("v", dst, d0 + 16 * n, win, w0, w1, "lst", c + n, c + 128)
+
+    def level(k, l, hooks):
+        v, tb = "v%d" % k, "tb%d" % l
+        w0, w1, ofs, ob, oa = ((2048, 4096, "abu", 0, 128) if l == 0 else (2048, 6144, "abu", 256, 384) if k == 1
+                               else (0, 4096, "abx", 0, 128))
+        for n in range(len(CUTS) - 1):
+            c0, c1 = CUTS[n], CUTS[n + 1]
+            gather("s", tb, 16 * c0, v, w0, w1, ofs, ob + c0, ob + c1, 255.0)
+            for fn in hooks.get(("b", n), []):
+                fn()
+            gather("v", v, 4096 + 2048 * l + 16 * c0, v, w0, w1, ofs, oa + c0, oa + c1, None, (tb, 16 * c0))
+            for fn in hooks.get(("a", n), []):
+                fn()
+
+    def votes(k, l):
+        v, vc = "v%d" % k, "vc%d" % l
+        o = 4096 + 2048 * l
+        def pack(b, src, s0, first):
+            def fn():
+                PE.matmul(T["pd%d" % b][:, 0:256], T.wp[:, 16:144], T[src][:, s0:s0 + 256], first, False)
+                return PE.matmul(T["pd%d" % b][:, 0:256], T.wp[:, 10:138], T[src][:, s0 + 256:s0 + 512], False, not first)
+            op("t", fn, [("wp", 0, 160), (src, s0, s0 + 512)], [("pd%d" % b, 0, 256)])
+        order = ((0, "v"), (2, "s"), (1, "v"), (3, "s"))
+        for b, q in order:
+            pack(b, v, o + 512 * b, True)
+        for b, q in order:
+            gather(q, vc, 512 * b, v, 2048, o + 2048, "cdu", 128 * l + 32 * b, 128 * l + 32 * b + 32, 0.0)
+            pack(b, vc, 512 * b, False)
+        for n, (b, q) in enumerate(order):
+            pd, a0 = "pd%d" % b, 256 * b
+            if q == "v":
+                vts("ad", a0, a0 + 256, pd, 0, 256, A.not_equal, 0.0)
+            else:
+                op("s", lambda: S.activation(T.ad[:, a0:a0 + 256], T[pd][:, 0:256], F.Abs), [(pd, 0, 256)], [("ad", a0, a0 + 256)])
+            def fn():
+                for m in range(2):
+                    c = WM + 15 - 4 * b - m
+                    ins = PE.matmul(T.pv[:, 0:128], T.ww[:, c:c + 128], T.ad[:, a0 + 128 * m:a0 + 128 * m + 128],
+                                    n == 0 and m == 0, n == 3 and m == 1)
+                return ins
+            op("t", fn, [("ww", WM, WM + 144), ("ad", a0, a0 + 256)], [("pv", 0, 128)])
+
+    def send_votes(k, l):
+        ph = 2 * (k - 1) + l
+        la, sg = "la%d" % ph, "sg%d" % ph
+        c0 = 128 * ph
+        vcp("cnt", c0, "pv", 0, 128)
+        exchange([(T[sg][:], T.cnt[:, c0:c0 + 128]), (T[la][r], T.cnt[16 * r:16 * r + 16, c0:c0 + 128])],
+                 ("cnt", c0, c0 + 128), (sg, 0, 1), lambda j: T[sg][j], la, "aa%d" % ph)
+
+    def window(k):
+        return ("v1", 2048) if k == 3 else ("win", 0)
+
+    def load_counts(k, l):
+        la = "la%d" % (2 * (k - 1) + l)
+        w, b = window(k)
+        c0 = b + 16 + 2048 * l
+        dma("y", [(T[w][16 * j:16 * j + 8, c0:c0 + 2048], T[la][:]) for j in range(8)], [(la, 0, 1)], [(w, c0, c0 + 2048)])
+
+    def load_cands(k):
+        w, b = window(k)
+        dma("y", [(T[w][16 * j + 8:16 * j + 10, b + 16:b + 4112], T.ctab[:]) for j in range(8)],
+            [("ctab", 0, 1)], [(w, b + 16, b + 4112)])
+
+    def pick(ps, p0, wt, src, s0, s1):
+        n = (s1 - s0) // 16
+        def fn():
+            for i in range(16):
+                c = wt + 15 - i
+                ins = PE.matmul(T[ps][:, p0:p0 + n], T.ww[:, c:c + 128], T[src][:, s0 + i:s1:16], i == 0, i == 15)
+            return ins
+        op("t", fn, [("ww", wt, wt + 144), (src, s0, s1)], [(ps, p0, p0 + n)])
+
+    def offsets(slot, a, b):
+        c = 32 * slot
+        vts("off", c + a, c + b, "stt", c + a, c + b, A.subtract, 2032.0, A.max, 15.0)
+
+    def look(qs, slot, k, l):
+        w, b = window(k)
+        per = 32 // len(qs)
+        for n, q in enumerate(qs):
+            o = 32 * slot + per * n
+            gather(q, "gq%d" % l, 16 * per * n, w, b, b + 16 + 2048 * (l + 1), "off", o, o + per)
+        pick("px%d" % l, 0, WC, "gq%d" % l, 0, 512)
+
+    def choose(slot, nxt, l):
+        px = "px%d" % l
+        c = 32 * slot
+        vtt("sm", 0, 16, px, 16, "stt", c + 16, A.min)
+        vtt("sm", 16, 16, px, 0, "stt", c + 16, A.subtract)
+        vtt("sm", 32, 16, "sm", 0, "sm", 16, A.add)
+        vtt("stt", 32 * nxt, 16, "sm", 32, "stt", c, A.min)
+
+    def share_list(slot, j):
+        vcp("su", 16 * j, "stt", 32 * slot, 16)
+        spread(T.su[:, 16 * j:16 * j + 16], ("su", 16 * j, 16 * j + 16), "lb%d" % j, "ab%d" % j)
+        offsets(slot, 0, 16)
+
+    def load_list(j):
+        c = 128 * (j + 1)
+        dma("y", [(T.lst[:, c:c + 128], T["lb%d" % j][:])], [("lb%d" % j, 0, 1)], [("lst", c, c + 128)])
+
+    def ahead_gather(slot, k, l):
+        w, b = window(k)
+        gather("s", "gp", 0, w, b, b + 16 + 2048 * (l + 1), "off", 32 * slot, 32 * slot + 16)
+        pick("pp", 0, WF, "gp", 0, 256)
+
+    def ahead_finish(slot):
+        c = 32 * slot
+        vtt("stt", c + 16, 16, "pp", 0, "stt", c, A.min)
+        offsets(slot, 16, 32)
+
+    def store_values(c0, c1):
+        dma("y", [(T.yv[:, c0:c1], T.v3[:, 2048 + c0:2048 + c1])], [("v3", 2048 + c0, 2048 + c1)], [])
+
+    def count_up(name, c0, n, step, base, cm):
+        kw = {} if SCRATCH[name][2] == "int32" else {"allow_small_or_imprecise_dtypes": True}
+        op("g", lambda: g.iota(T[name][:, c0:c0 + n], [[step, n]], base, cm, **kw), [], [(name, c0, c0 + n)])
+
+    def keep(name, c0, s0, n, pattern, cmp, other, base, cm):
+        op("g", lambda: g.affine_select(T[name][:, c0:c0 + n], T[name][:, s0:s0 + n], pattern, cmp, other, base, cm),
+           [(name, s0, s0 + n)], [(name, c0, c0 + n)])
+
+    def woven(at, old, new, k, j):
+        return {("b", at): [lambda: look("vs", old, k, 0)],
+                ("a", at + 1): [lambda: choose(old, new, 0), lambda: share_list(new, j)]}
+
+    R0, R1, R2, T0, T1, T2, R3, T3 = range(8)
+
+    dma("y", [(T.ab[:, 0:128], T.fb[:, 0:128])], [], [("ab", 0, 128)])
+    dma("s", [(T.cdi[:], T.cd[:])], [], [("cdi", 0, 256)])
+    dma("y", [(T.ab[:, 128:256], T.fa[:, 0:128])], [], [("ab", 128, 256)])
+    dma("s", [(T.v1[:, 2048:4096], T.x[:])], [], [("v1", 2048, 4096)])
+    dma("y", [(T.ab[:, 256:384], T.fb[:, 128:256]), (T.ab[:, 384:512], T.fa[:, 128:256])], [], [("ab", 256, 512)])
+    dma("y", [(T.tpi[:], T.tp[:]), (T.own[:, 0:16], T.cd[16 * r:16 * r + 16, 0:128]),
+              (T.own[:, 16:32], T.tp[16 * r:16 * r + 16, 0:128])], [], [("tpi", 0, 128), ("own", 0, 32)])
+    fill("win", 16, 4112, 0.0)
+    fill("win", 0, 16, BIG / 2)
+    fill("ww", 0, 576, 0.0)
+    count_up("sel", 0, 16, 0, 1, 0)
+    count_up("bnd", 32, 8, 0, 1, 0)
+    count_up("bnd", 0, 8, 0, BIG, 0)
+    keep("sel", 0, 0, 16, [[-1, 16]], A.is_equal, 0.0, -16 * r, 1)
+    keep("bnd", 0, 0, 8, [[16, 8]], A.is_ge, 1.0, 7, -1)
+    for c, lo in ((8, 8), (16, 0), (24, 6), (40, 0), (0, 0)):
+        keep("bnd", c, 32 if c else 0, 8, [[-16, 8]], A.is_ge, 0.0, -lo, 1)
+    for c, hi in ((8, 9), (16, 5), (24, 15), (40, 15), (0, 9)):
+        keep("bnd", c, c, 8, [[16, 8]], A.is_ge, 0.0, hi, -1)
+    count_up("wp", 0, 16, 0, 0, 0)
+    count_up("wp", 16, 144, 0, 65536, 0)
+    keep("wp", 16, 16, 144, [[-16, 9], [-3, 16]], A.is_ge, 256.0, -2, 1)
+    keep("wp", 16, 16, 144, [[-16, 9], [-3, 16]], A.is_ge, 1.0, -1, 1)
+    keep("wp", 16, 16, 144, [[-16, 9], [-3, 16]], A.is_ge, 0.0, 0, 1)
+    keep("wp", 16, 16, 144, [[16, 9], [3, 16]], A.is_ge, 0.0, 2, -1)
+    keep("wp", 16, 16, 144, [[16, 9], [0, 16]], A.is_ge, 0.0, 15, -1)
+    count_up("ti", 0, 16, 16, 2048, 256)
+    count_up("pi", 0, 4, 0, 0, 1)
+    vcp("abu", 0, "ab", 0, 128)
+    vcp("cdf", 0, "cdi", 0, 256)
+    vcp("cdu", 0, "cdi", 0, 256)
+
+    def turn():
+        PE.matmul(T.pp[:, 0:16], T.cdf[:, 0:256:2], T.sel[:, 0:16], True, True)
+        return PE.matmul(T.pp[:, 16:32], T.cdf[:, 1:256:2], T.sel[:, 0:16], True, True)
+    op("t", turn, [("cdf", 0, 256), ("sel", 0, 16)], [("pp", 0, 32)])
+    vcp("abu", 128, "ab", 128, 128)
+    vcp("chl", 0, "pp", 0, 32)
+    for c, s in ((WC + 15, 0), (WF + 15, 8), (WM + 15, 16), (WM + 17, 24), (WE + 15, 40)):
+        vcp("ww", c, "bnd", s, 8, 16)
+    vtt("chl", 32, 32, "pp", 0, "chl", 0, A.subtract)
+    dma("y", [(T.ctab[0], T.chl[:, 0:32]), (T.ctab[1], T.chl[:, 32:64])], [("chl", 0, 64)], [("ctab", 0, 1)])
+    load_cands(1)
+
+    level(1, 0, {})
+    votes(1, 0)
+    vcp("abu", 256, "ab", 256, 256)
+    vcp("stt", 32 * T0, "own", 16, 16)
+    send_votes(1, 0)
+    offsets(T0, 0, 16)
+    vcp("lst", 0, "tpi", 0, 128)
+    level(1, 1, {})
+    ahead_gather(T0, 1, 1)
+    load_counts(1, 0)
+    votes(1, 1)
+    ahead_finish(T0)
+    shared("v2", 2048, "v1", 2048, 8192, 0, SHARE)
+    send_votes(1, 1)
+    fill("v1", 2048, 2064, BIG / 2)
+    load_cands(3)
+    vts("pj", 0, 4, "pi", 0, 4, A.arith_shift_right, 3)
+    vcp("stt", 32 * R0 + 16, "own", 0, 16)
+    vts("pk", 0, 4, "pj", 0, 4, A.mult, -2047.0)
+    vts("w1", 0, 256, "ab", 256, 512, A.add, 2048.0)
+    op("v", lambda: V.tensor_scalar(T.stt[:, 0:16], T.ti[:, 0:16], T.pk[:, 0:1], None, A.add),
+       [("ti", 0, 16), ("pk", 0, 4)], [("stt", 0, 16)])
+
+    hooks = woven(LOOK1, R0, R1, 1, 0)
+    hooks[("a", 0)] = [lambda: offsets(R0, 0, 32)]
+    level(2, 0, hooks)
+    ahead_gather(R1, 3, 0)
+    load_counts(1, 1)
+    votes(2, 0)
+    vts("aby", 0, 256, "w1", 0, 256, A.bitwise_and, 4095)
+    send_votes(2, 0)
+    load_list(0)
+    look("vs", T0, 1, 1)
+    vcp("abx", 0, "aby", 0, 256)
+    ahead_finish(R1)
+    choose(T0, T1, 1)
+    share_list(T1, 1)
+    load_counts(2, 0)
+    shared("v2", 0, "v2", 2048, 6144, 128, SHARE2)
+    load_list(1)
+    level(2, 1, woven(LOOK2, R1, R2, 2, 2))
+    ahead_gather(T1, 3, 1)
+
+    shared("v3", 2048, "v2", 2048, 8192, 256, SHARE)
+    ahead_finish(T1)
+    dma("y", [(T.tw[:], T.v2[:, 6144:8192])], [("v2", 6144, 8192)], [("tw", 0, 2048)])
+    load_list(2)
+    store_values(0, 2048)
+    level(3, 0, {})
+    ahead_gather(R2, 3, 0)
+    votes(3, 0)
+    ahead_finish(R2)
+    send_votes(3, 0)
+    store_values(2048, 4096)
+    gather("s", "v3", 0, "v3", 2048, 6144, "lst", 384, 512)
+    gather("v", "vc1", 0, "v2", 2048, 8192, "cdu", 128, 256, None, ("tw", 0), A.not_equal)
+    def plain():
+        for i in range(16):
+            c = WE + 15 - i
+            ins = PE.matmul(T.pv[:, 0:128], T.ww[:, c:c + 128], T.vc1[:, 128 * i:128 * i + 128], i == 0, i == 15)
+        return ins
+    op("t", plain, [("ww", WE, WE + 144), ("vc1", 0, 2048)], [("pv", 0, 128)])
+    level(3, 1, {("a", 0): [lambda: send_votes(2, 1)], ("a", 1): [lambda: load_counts(3, 0)]})
+    store_values(4096, 6144)
+    load_counts(2, 1)
+    votes(3, 1)
+    send_votes(3, 1)
+
+    look("vs", R2, 3, 0)
+    choose(R2, R3, 0)
+    c = 32 * R3
+    vcp("sb", 0, "stt", c, 16, 2)
+    op("v", lambda: V.tensor_tensor(T.sb[:, 1:32:2], T.stt[:, c:c + 16], T.sb[:, 0:32:2], A.subtract),
+       [("stt", c, c + 16), ("sb", 0, 32)], [("sb", 0, 32)])
+    spread(T.sb[:, 0:32], ("sb", 0, 32), "lb3", "ab3")
+    look("s", T1, 2, 1)
+    fill("v2", 6144, 6160, BIG / 2)
+    vts("w1", 0, 256, "aby", 0, 256, A.bitwise_and, 15)
+    vts("w3", 0, 256, "aby", 0, 256, A.is_ge, 2048.0, A.mult, 65536.0)
+    vts("w2", 0, 256, "w1", 0, 256, A.mult, 2047.0)
+    choose(T1, T2, 1)
+    offsets(T2, 0, 16)
+    ahead_gather(T2, 2, 1)
+    vtt("w3", 0, 256, "w3", 0, "aby", 0, A.add)
+    vcp("abf", 0, "ab", 0, 512)
+    ahead_finish(T2)
+    vtt("w3", 0, 256, "w3", 0, "w2", 0, A.add)
+    vts("abz", 0, 256, "w3", 0, 256, A.mult, 0.125, A.min, 4096.0)
+    load_counts(3, 1)
+    dma("s", [(T.v2[8:128:16, 2048:6144], T.lb3[:]), (T.v2[9:128:16, 2047:6143], T.lb3[:])], [("lb3", 0, 1)],
+        [("v2", 2047, 6144)])
+    look("vs", T2, 3, 1)
+    choose(T2, T3, 1)
+    c3 = 32 * T3
+    dma("y", [(T.yb[:, 0:128], T.abf[:, 0:128]), (T.ya[:, 0:128], T.abf[:, 128:256])], [("abf", 0, 256)], [])
+    spread(T.stt[:, c3:c3 + 16], ("stt", c3, c3 + 16), "lb4", "ab4")
+    gather("s", "tb1", 0, "v2", 2048, 6160, "abz", 0, 64)
+    gather("v", "tb0", 1024, "v2", 2048, 6160, "abz", 192, 256)
+    gather("s", "tb1", 1024, "v2", 2048, 6160, "abz", 64, 128)
+    gather("v", "tb0", 16 * LAST, "v2", 2048, 6160, "abz", 128 + LAST, 192)
+    gather("s", "tb0", 0, "v2", 2048, 6160, "abz", 128, 128 + LAST)
+    pick("pv", 0, WF, "tb1", 0, 1024)
+    pick("px0", 64, WF, "tb0", 1024, 2048)
+    pick("pv", 64, WF, "tb1", 1024, 2048)
+    pick("px0", 0, WF, "tb0", 0, 1024)
+    vtt("abf", 256, 128, "pv", 0, "abf", 256, A.min)
+    dma("s", [(T.yb[:, 128:256], T.abf[:, 256:384])], [("abf", 256, 384)], [])
+    vtt("abf", 384, 128, "px0", 0, "abf", 384, A.min)
+    dma("s", [(T.ya[:, 128:256], T.abf[:, 384:512])], [("abf", 384, 512)], [])
+    dma("y", [(T.yt[:], T.lb4[:])], [("lb4", 0, 1)], [])
+    for s in total:
+        if known["g"].get(s, 0) < total[s]:
+            g.wait_ge(T.sem[s], total[s])

@@ -1,12 +1,11 @@
 from concourse.bass import DstId, RemoteDMATransfer
 from concourse.mybir import AluOpType, ActivationFunctionType
 
-SHARE = 68
-SHARE2 = 72
+SHARE = [104, 68, 80, 88]
+SPLIT = [88, 92, 84, 0, 80, 80]
+HELP = 12
 LAST = 16
-LOOK1 = 2
-LOOK2 = 3
-STAGE2 = True
+LOOK = 1
 BIG = 8192
 CUTS = [0, 26, 52, 78, 104, 128]
 
@@ -166,8 +165,8 @@ def rank_program(g, core, T, topo):
     plans = {c: deal_engines(c, cores, topo) for c in cores}
     arrive = sum(len(plans[c][core]) for c in cores if c != core)
 
-    def exchange(pairs, reg, source, src_of, land, sem):
-        dma("y", pairs, [reg], [(land, 0, 1)] + ([source] if source != reg else []))
+    def exchange(pairs, reg, source, src_of, land, sem, q="y"):
+        dma(q, pairs, [reg], [(land, 0, 1), source])
         def send():
             trs = []
             for k, c in enumerate(cores):
@@ -184,10 +183,7 @@ def rank_program(g, core, T, topo):
         recs.append(("far", [], [span((land, 0, 1))], sem, arrive, {sem: arrive}))
 
     def spread(src, reg, land, sem):
-        if STAGE2:
-            exchange([(T[land][r], src)], reg, (land, 0, 1), lambda k: T[land][r], land, sem)
-        else:
-            exchange([(T[land][r], src)], reg, reg, lambda k: src, land, sem)
+        exchange([(T[land][r], src)], reg, (land, 0, 1), lambda k: T[land][r], land, sem)
 
     def vts(dst, d0, d1, src, s0, s1, *ops):
         a = (ops[1], None, ops[0]) if len(ops) == 2 else (ops[1], ops[3], ops[0], ops[2])
@@ -200,6 +196,9 @@ def rank_program(g, core, T, topo):
     def vcp(dst, d0, src, s0, n, step=1):
         d1 = d0 + step * (n - 1) + 1
         op("v", lambda: V.tensor_copy(T[dst][:, d0:d1:step], T[src][:, s0:s0 + n]), [(src, s0, s0 + n)], [(dst, d0, d1)])
+
+    def act(dst, d0, src, n, func):
+        op("s", lambda: S.activation(T[dst][:, d0:d0 + n], T[src][:, 0:n], func), [(src, 0, n)], [(dst, d0, d0 + n)])
 
     def fill(dst, d0, d1, value):
         op("v", lambda: V.memset(T[dst][:, d0:d1], value), [], [(dst, d0, d1)])
@@ -222,24 +221,28 @@ def rank_program(g, core, T, topo):
             fn = lambda: S.activation(out, src, F.Copy)
         op(q, fn, reads, [(dst, d0, d0 + n)])
 
-    def shared(dst, d0, win, w0, w1, c, n):
+    def shared(dst, d0, win, w0, w1, j):
+        c, n = 128 * j, SHARE[j]
         gather("s", dst, d0, win, w0, w1, "lst", c, c + n)
         gather("v", dst, d0 + 16 * n, win, w0, w1, "lst", c + n, c + 128)
 
-    def level(k, l, hooks):
+    def level(k, l, hooks, own=HELP):
         v, tb = "v%d" % k, "tb%d" % l
         w0, w1, ofs, ob, oa = ((2048, 4096, "abu", 0, 128) if l == 0 else (2048, 6144, "abu", 256, 384) if k == 1
                                else (0, 4096, "abx", 0, 128))
         for n in range(len(CUTS) - 1):
             c0, c1 = CUTS[n], CUTS[n + 1]
-            gather("s", tb, 16 * c0, v, w0, w1, ofs, ob + c0, ob + c1, 255.0)
+            h = c1 - own if n == 0 else c1
+            gather("s", tb, 16 * c0, v, w0, w1, ofs, ob + c0, ob + h, 255.0)
+            if h < c1:
+                gather("v", tb, 16 * h, v, w0, w1, ofs, ob + h, ob + c1, 255.0)
             for fn in hooks.get(("b", n), []):
                 fn()
             gather("v", v, 4096 + 2048 * l + 16 * c0, v, w0, w1, ofs, oa + c0, oa + c1, None, (tb, 16 * c0))
             for fn in hooks.get(("a", n), []):
                 fn()
 
-    def votes(k, l):
+    def votes(k, l, who, gap=None):
         v, vc = "v%d" % k, "vc%d" % l
         o = 4096 + 2048 * l
         def pack(b, src, s0, first):
@@ -247,33 +250,44 @@ def rank_program(g, core, T, topo):
                 PE.matmul(T["pd%d" % b][:, 0:256], T.wp[:, 16:144], T[src][:, s0:s0 + 256], first, False)
                 return PE.matmul(T["pd%d" % b][:, 0:256], T.wp[:, 10:138], T[src][:, s0 + 256:s0 + 512], False, not first)
             op("t", fn, [("wp", 0, 160), (src, s0, s0 + 512)], [("pd%d" % b, 0, 256)])
-        order = ((0, "v"), (2, "s"), (1, "v"), (3, "s"))
-        for b, q in order:
+        def part(q, c0, c1):
+            gather(q, vc, 16 * c0, v, 2048, o + 16 * c1, "cdu", 128 * l + c0, 128 * l + c1, 0.0)
+        cut = SPLIT[2 * (k - 1) + l]
+        for b in range(2):
             pack(b, v, o + 512 * b, True)
-        for b, q in order:
-            gather(q, vc, 512 * b, v, 2048, o + 2048, "cdu", 128 * l + 32 * b, 128 * l + 32 * b + 32, 0.0)
+            part("s", 32 * b, 32 * b + 32)
             pack(b, vc, 512 * b, False)
-        for n, (b, q) in enumerate(order):
+        part("s", 64, cut)
+        part("v", cut, 128)
+        for first in (True, False):
+            for b in (2, 3):
+                pack(b, v if first else vc, (o if first else 0) + 512 * b, first)
+        for b in range(4):
             pd, a0 = "pd%d" % b, 256 * b
-            if q == "v":
+            if b == 2 and gap:
+                gap()
+            if who[b] == "v":
                 vts("ad", a0, a0 + 256, pd, 0, 256, A.not_equal, 0.0)
             else:
-                op("s", lambda: S.activation(T.ad[:, a0:a0 + 256], T[pd][:, 0:256], F.Abs), [(pd, 0, 256)], [("ad", a0, a0 + 256)])
+                act("ad", a0, pd, 256, F.Abs)
             def fn():
                 for m in range(2):
                     c = WM + 15 - 4 * b - m
                     ins = PE.matmul(T.pv[:, 0:128], T.ww[:, c:c + 128], T.ad[:, a0 + 128 * m:a0 + 128 * m + 128],
-                                    n == 0 and m == 0, n == 3 and m == 1)
+                                    b == 0 and m == 0, b == 3 and m == 1)
                 return ins
             op("t", fn, [("ww", WM, WM + 144), ("ad", a0, a0 + 256)], [("pv", 0, 128)])
 
-    def send_votes(k, l):
+    def send_votes(k, l, q):
         ph = 2 * (k - 1) + l
         la, sg = "la%d" % ph, "sg%d" % ph
         c0 = 128 * ph
-        vcp("cnt", c0, "pv", 0, 128)
+        if q == "v":
+            vcp("cnt", c0, "pv", 0, 128)
+        else:
+            act("cnt", c0, "pv", 128, F.Copy)
         exchange([(T[sg][:], T.cnt[:, c0:c0 + 128]), (T[la][r], T.cnt[16 * r:16 * r + 16, c0:c0 + 128])],
-                 ("cnt", c0, c0 + 128), (sg, 0, 1), lambda j: T[sg][j], la, "aa%d" % ph)
+                 ("cnt", c0, c0 + 128), (sg, 0, 1), lambda j: T[sg][j], la, "aa%d" % ph, "y" if q == "v" else "s")
 
     def window(k):
         return ("v1", 2048) if k == 3 else ("win", 0)
@@ -348,16 +362,12 @@ def rank_program(g, core, T, topo):
         op("g", lambda: g.affine_select(T[name][:, c0:c0 + n], T[name][:, s0:s0 + n], pattern, cmp, other, base, cm),
            [(name, s0, s0 + n)], [(name, c0, c0 + n)])
 
-    def woven(at, old, new, k, j):
-        return {("b", at): [lambda: look("vs", old, k, 0)],
-                ("a", at + 1): [lambda: choose(old, new, 0), lambda: share_list(new, j)]}
-
     R0, R1, R2, T0, T1, T2, R3, T3 = range(8)
 
     dma("y", [(T.ab[:, 0:128], T.fb[:, 0:128])], [], [("ab", 0, 128)])
-    dma("s", [(T.cdi[:], T.cd[:])], [], [("cdi", 0, 256)])
-    dma("y", [(T.ab[:, 128:256], T.fa[:, 0:128])], [], [("ab", 128, 256)])
+    dma("s", [(T.ab[:, 128:256], T.fa[:, 0:128])], [], [("ab", 128, 256)])
     dma("s", [(T.v1[:, 2048:4096], T.x[:])], [], [("v1", 2048, 4096)])
+    dma("y", [(T.cdi[:], T.cd[:])], [], [("cdi", 0, 256)])
     dma("y", [(T.ab[:, 256:384], T.fb[:, 128:256]), (T.ab[:, 384:512], T.fa[:, 128:256])], [], [("ab", 256, 512)])
     dma("y", [(T.tpi[:], T.tp[:]), (T.own[:, 0:16], T.cd[16 * r:16 * r + 16, 0:128]),
               (T.own[:, 16:32], T.tp[16 * r:16 * r + 16, 0:128])], [], [("tpi", 0, 128), ("own", 0, 32)])
@@ -382,36 +392,32 @@ def rank_program(g, core, T, topo):
     keep("wp", 16, 16, 144, [[16, 9], [0, 16]], A.is_ge, 0.0, 15, -1)
     count_up("ti", 0, 16, 16, 2048, 256)
     count_up("pi", 0, 4, 0, 0, 1)
-    vcp("abu", 0, "ab", 0, 128)
-    vcp("cdf", 0, "cdi", 0, 256)
-    vcp("cdu", 0, "cdi", 0, 256)
+    vcp("abu", 0, "ab", 0, 256)
+    for c, s in ((WC + 15, 0), (WF + 15, 8), (WM + 15, 16), (WM + 17, 24), (WE + 15, 40)):
+        vcp("ww", c, "bnd", s, 8, 16)
 
     def turn():
         PE.matmul(T.pp[:, 0:16], T.cdf[:, 0:256:2], T.sel[:, 0:16], True, True)
         return PE.matmul(T.pp[:, 16:32], T.cdf[:, 1:256:2], T.sel[:, 0:16], True, True)
-    op("t", turn, [("cdf", 0, 256), ("sel", 0, 16)], [("pp", 0, 32)])
-    vcp("abu", 128, "ab", 128, 128)
-    vcp("chl", 0, "pp", 0, 32)
-    for c, s in ((WC + 15, 0), (WF + 15, 8), (WM + 15, 16), (WM + 17, 24), (WE + 15, 40)):
-        vcp("ww", c, "bnd", s, 8, 16)
-    vtt("chl", 32, 32, "pp", 0, "chl", 0, A.subtract)
-    dma("y", [(T.ctab[0], T.chl[:, 0:32]), (T.ctab[1], T.chl[:, 32:64])], [("chl", 0, 64)], [("ctab", 0, 1)])
-    load_cands(1)
+    def split():
+        vcp("chl", 0, "pp", 0, 32)
+        vtt("chl", 32, 32, "pp", 0, "chl", 0, A.subtract)
+        dma("y", [(T.ctab[0], T.chl[:, 0:32]), (T.ctab[1], T.chl[:, 32:64])], [("chl", 0, 64)], [("ctab", 0, 1)])
+        load_cands(1)
 
-    level(1, 0, {})
-    votes(1, 0)
-    vcp("abu", 256, "ab", 256, 256)
-    vcp("stt", 32 * T0, "own", 16, 16)
-    send_votes(1, 0)
-    offsets(T0, 0, 16)
-    vcp("lst", 0, "tpi", 0, 128)
-    level(1, 1, {})
-    ahead_gather(T0, 1, 1)
+    level(1, 0, {("a", 2): [lambda: vcp("cdu", 0, "cdi", 0, 256)]})
+    vcp("abu", 256, "ab", 256, 128)
+    votes(1, 0, "vvvv", lambda: vcp("abu", 384, "ab", 384, 128))
+    vcp("cdf", 0, "cdi", 0, 256)
+    send_votes(1, 0, "v")
+    op("t", turn, [("cdf", 0, 256), ("sel", 0, 16)], [("pp", 0, 32)])
+    level(1, 1, {("a", 0): [split]}, 0)
     load_counts(1, 0)
-    votes(1, 1)
-    ahead_finish(T0)
-    shared("v2", 2048, "v1", 2048, 8192, 0, SHARE)
-    send_votes(1, 1)
+    vcp("lst", 0, "tpi", 0, 128)
+    votes(1, 1, "vvvv")
+    vcp("stt", 32 * T0, "own", 16, 16)
+    shared("v2", 2048, "v1", 2048, 8192, 0)
+    send_votes(1, 1, "v")
     fill("v1", 2048, 2064, BIG / 2)
     load_cands(3)
     vts("pj", 0, 4, "pi", 0, 4, A.arith_shift_right, 3)
@@ -421,52 +427,54 @@ def rank_program(g, core, T, topo):
     op("v", lambda: V.tensor_scalar(T.stt[:, 0:16], T.ti[:, 0:16], T.pk[:, 0:1], None, A.add),
        [("ti", 0, 16), ("pk", 0, 4)], [("stt", 0, 16)])
 
-    hooks = woven(LOOK1, R0, R1, 1, 0)
-    hooks[("a", 0)] = [lambda: offsets(R0, 0, 32)]
-    level(2, 0, hooks)
-    ahead_gather(R1, 3, 0)
+    offsets(R0, 0, 32)
+    offsets(T0, 0, 16)
+    level(2, 0, {("b", LOOK): [lambda: look("vs", R0, 1, 0)],
+                 ("a", LOOK + 1): [lambda: choose(R0, R1, 0), lambda: share_list(R1, 0)]}, 0)
     load_counts(1, 1)
-    votes(2, 0)
+    ahead_gather(T0, 3, 1)
+    votes(2, 0, "svvs", lambda: ahead_finish(T0))
     vts("aby", 0, 256, "w1", 0, 256, A.bitwise_and, 4095)
-    send_votes(2, 0)
     load_list(0)
-    look("vs", T0, 1, 1)
+    send_votes(2, 0, "s")
+    look("v", T0, 1, 1)
+    ahead_gather(R1, 3, 0)
     vcp("abx", 0, "aby", 0, 256)
-    ahead_finish(R1)
     choose(T0, T1, 1)
     share_list(T1, 1)
     load_counts(2, 0)
-    shared("v2", 0, "v2", 2048, 6144, 128, SHARE2)
+    shared("v2", 0, "v2", 2048, 6144, 1)
     load_list(1)
-    level(2, 1, woven(LOOK2, R1, R2, 2, 2))
-    ahead_gather(T1, 3, 1)
+    level(2, 1, {("a", 0): [lambda: ahead_finish(R1)], ("b", 4): [lambda: look("vs", R1, 2, 0)]})
+    choose(R1, R2, 0)
+    share_list(R2, 2)
 
-    shared("v3", 2048, "v2", 2048, 8192, 256, SHARE)
-    ahead_finish(T1)
+    shared("v3", 2048, "v2", 2048, 8192, 2)
     dma("y", [(T.tw[:], T.v2[:, 6144:8192])], [("v2", 6144, 8192)], [("tw", 0, 2048)])
     load_list(2)
     store_values(0, 2048)
     level(3, 0, {})
     ahead_gather(R2, 3, 0)
-    votes(3, 0)
-    ahead_finish(R2)
-    send_votes(3, 0)
+    votes(3, 0, "ssss")
+    send_votes(3, 0, "s")
     store_values(2048, 4096)
-    gather("s", "v3", 0, "v3", 2048, 6144, "lst", 384, 512)
     gather("v", "vc1", 0, "v2", 2048, 8192, "cdu", 128, 256, None, ("tw", 0), A.not_equal)
+    ahead_finish(R2)
+    shared("v3", 0, "v3", 2048, 6144, 3)
     def plain():
         for i in range(16):
             c = WE + 15 - i
             ins = PE.matmul(T.pv[:, 0:128], T.ww[:, c:c + 128], T.vc1[:, 128 * i:128 * i + 128], i == 0, i == 15)
         return ins
     op("t", plain, [("ww", WE, WE + 144), ("vc1", 0, 2048)], [("pv", 0, 128)])
-    level(3, 1, {("a", 0): [lambda: send_votes(2, 1)], ("a", 1): [lambda: load_counts(3, 0)]})
+    level(3, 1, {("a", 0): [lambda: send_votes(2, 1, "v")], ("a", 1): [lambda: load_counts(3, 0)]})
+    ahead_gather(T1, 2, 1)
     store_values(4096, 6144)
     load_counts(2, 1)
-    votes(3, 1)
-    send_votes(3, 1)
+    votes(3, 1, "svvs", lambda: ahead_finish(T1))
+    send_votes(3, 1, "s")
 
-    look("vs", R2, 3, 0)
+    look("v", R2, 3, 0)
     choose(R2, R3, 0)
     c = 32 * R3
     vcp("sb", 0, "stt", c, 16, 2)

@@ -1,98 +1,104 @@
 from concourse.bass import DstId, RemoteDMATransfer
 from concourse.mybir import AluOpType, ActivationFunctionType
 
-SHARE = [104, 68, 80, 88]
-SPLIT = [88, 92, 84, 0, 80, 80]
-HELP = 12
-LAST = 16
-LOOK = 1
 BIG = 8192
-CUTS = [0, 26, 52, 78, 104, 128]
+CUTS = [[0, 32, 64, 96, 128], [0, 32, 64, 96, 128], [0, 32, 64, 96, 128], [0, 28, 64, 100, 128], [0, 32, 64, 96, 128],
+        [0, 20, 44, 68, 96, 128]]
+HELP = [22, 4, 8, 16, 22, 26]
+PACK = [((4, 6, 6), "vvs"), ((4, 4, 6), "vvv"), ((3, 5, 6), "svv"), ((3, 4, 6), ""), ((3, 7, 7), "sss"),
+        ((4, 6, 7), "vvv")]
+SHARE = [88, 72, 64, 84]
+STAGE = [True, False]
+LATE = [3, 5, 6]
+DQ = ["y", "y", "y", "y", "y", "y", "y", "ys", "y", "y", "s"]
+LQ = ["vs", "s", "v", "v", "v", "s", "v", "s", "v", "s", "s"]
+PLACES = {
+    "b10.0": "cand0 candf", "a10.2": "turn", "a10.3": "fanb1 fana1 taps0", "c10.0": "cand1", "e10": "sum10.0",
+    "b11.0": "sum10.1 sum10.2 tapf", "b11.1": "send10 table", "x0v": "sum11.0 sum11.1 sum11.2 first table3",
+    "b20.0": "load10", "a20.0": "send11 again2", "b20.1": "load11", "b20.2": "lookR0", "a20.2": "shareR1",
+    "b20.3": "aheadT0", "c20.0": "candT0", "e20": "sum20.0 sum20.1 sum20.2 send20 listR1 lookT0", "x1s": "shareT1",
+    "x1v": "aheadR1", "b21.0": "candR1", "a21.1": "load20", "b21.3": "listT1", "a21.3": "lookR1", "x2v": "shareR2",
+    "b30.2": "aheadR2", "b30.3": "again3 twin", "a30.3": "store0", "p30": "late0 late1 late2 listR2",
+    "c30.0": "store1", "e30": "sum30.0 sum30.1 sum30.2 late3 send30", "x3v": "send21 candR2", "b31.0": "flatT1",
+    "b31.1": "load30", "a31.3": "store2", "a31.4": "fin3", "p31": "stateT1", "e31": "aheadT1 store3",
+    "end0": "sum31.0 sum31.1 sum31.2 load21 send31 lookR2 candT1 lookT1 fin2", "end1": "shareR3",
+    "end2": "fin0 stateT2 aheadT2", "end3": "candT2", "end4": "fin1", "end5": "load31 rowsR3 lookT2 shareT3 out0"}
+PLAN = {name: place for place in PLACES for name in PLACES[place].split()}
 
 SCRATCH = {
     "v1": ("sbuf", [128, 8192], "bfloat16"),
     "v2": ("sbuf", [128, 8192], "bfloat16"),
     "v3": ("sbuf", [128, 8192], "bfloat16"),
     "win": ("sbuf", [128, 4112], "bfloat16"),
-    "tw": ("sbuf", [128, 2048], "bfloat16"),
-    "ad": ("sbuf", [128, 1024], "bfloat16"),
+    "ad": ("sbuf", [128, 768], "bfloat16"),
     "ab": ("sbuf", [128, 512], "int32"),
     "abu": ("sbuf", [128, 512], "uint16"),
     "abf": ("sbuf", [128, 512], "float32"),
-    "aby": ("sbuf", [128, 256], "int32"),
-    "abx": ("sbuf", [128, 256], "uint16"),
+    "xu": ("sbuf", [128, 4096], "bfloat16"),
     "abz": ("sbuf", [128, 256], "uint16"),
     "w1": ("sbuf", [128, 256], "int32"),
-    "w2": ("sbuf", [128, 256], "float32"),
-    "w3": ("sbuf", [128, 256], "float32"),
     "cdi": ("sbuf", [128, 256], "int32"),
     "cdu": ("sbuf", [128, 256], "uint16"),
     "cdf": ("sbuf", [128, 256], "float32"),
     "tpi": ("sbuf", [128, 128], "int32"),
     "lst": ("sbuf", [128, 512], "uint16"),
-    "own": ("sbuf", [128, 32], "int32"),
     "chl": ("sbuf", [128, 64], "bfloat16"),
-    "ww": ("sbuf", [128, 576], "bfloat16"),
-    "wp": ("sbuf", [128, 160], "bfloat16"),
-    "bnd": ("sbuf", [128, 48], "bfloat16"),
+    "tw": ("sbuf", [128, 2048], "bfloat16"),
+    "ww": ("sbuf", [128, 864], "bfloat16"),
+    "wp": ("sbuf", [128, 304], "bfloat16"),
+    "bnd": ("sbuf", [128, 160], "bfloat16"),
     "sel": ("sbuf", [128, 16], "float32"),
-    "ti": ("sbuf", [128, 16], "float32"),
-    "pi": ("sbuf", [128, 4], "int32"),
-    "pj": ("sbuf", [128, 4], "int32"),
-    "pk": ("sbuf", [128, 4], "float32"),
-    "stt": ("sbuf", [128, 256], "float32"),
+    "eye": ("sbuf", [128, 128], "float32"),
+    "tpf": ("sbuf", [128, 128], "float32"),
+    "stt": ("sbuf", [128, 32], "float32"),
+    "dd": ("sbuf", [128, 384], "float32"),
     "off": ("sbuf", [128, 192], "uint16"),
-    "sm": ("sbuf", [128, 48], "float32"),
+    "oa": ("sbuf", [128, 96], "uint16"),
+    "sm": ("sbuf", [128, 128], "float32"),
     "gp": ("sbuf", [128, 256], "bfloat16"),
     "cnt": ("sbuf", [128, 768], "bfloat16"),
-    "su": ("sbuf", [128, 48], "uint16"),
+    "su": ("sbuf", [128, 16], "uint16"),
     "sb": ("sbuf", [128, 32], "bfloat16"),
     "ctab": ("dram", [2, 128, 32], "bfloat16"),
-    "lb0": ("dram", [8, 128, 16], "uint16"),
-    "lb1": ("dram", [8, 128, 16], "uint16"),
-    "lb2": ("dram", [8, 128, 16], "uint16"),
+    "ln0": ("sbuf", [128, 128], "float32"),
+    "ln1": ("sbuf", [128, 128], "float32"),
+    "ln2": ("sbuf", [128, 128], "float32"),
     "lb3": ("dram", [8, 128, 32], "bfloat16"),
     "lb4": ("dram", [8, 128, 16], "float32"),
     "pp": ("psum", [128, 512], "float32"),
-    "pv": ("psum", [128, 512], "float32"),
+    "pl": ("psum", [128, 512], "float32"),
 }
 for _k in range(2):
     for _n in ("tb", "vc"):
         SCRATCH["%s%d" % (_n, _k)] = ("sbuf", [128, 2048], "bfloat16")
     SCRATCH["gq%d" % _k] = ("sbuf", [128, 512], "bfloat16")
-    SCRATCH["px%d" % _k] = ("psum", [128, 512], "float32")
-for _k in range(4):
-    SCRATCH["pd%d" % _k] = ("psum", [128, 512], "float32")
+for _n in ("px0", "px1", "pd0", "pd1", "pd2", "pv"):
+    SCRATCH[_n] = ("psum", [128, 512], "float32")
 for _k in range(6):
     SCRATCH["la%d" % _k] = ("dram", [8, 128, 16], "bfloat16")
     SCRATCH["sg%d" % _k] = ("dram", [8, 128, 16], "bfloat16")
 
 SEMAPHORES = (["cv", "cs", "ct", "cg", "loc"] + ["aa%d" % k for k in range(6)] + ["ab%d" % k for k in range(5)]
-              + ["d%d" % k for k in range(48)])
+              + ["d%d" % k for k in range(80)])
 SIZE = {"bfloat16": 2, "uint16": 2, "float32": 4, "int32": 4}
 A = AluOpType
 F = ActivationFunctionType
-WC, WF, WM, WE = 0, 144, 288, 432
+WC, WF, WS, WE = 0, 144, 288, 720
 
 
-def deal_engines(src, cores, topo):
+def deal_engines(src, cores, topo, many):
     far = [c for c in cores if topo.chip(c) != topo.chip(src)]
     near = [c for c in cores if c != src and topo.chip(c) == topo.chip(src)]
-    out = {}
-    used = []
-    for group in (far, near):
-        if not group:
-            continue
-        pool = [e for e in topo.engines(src, group[0]) if e not in used]
-        for n, c in enumerate(group):
-            left = len(group) - n
-            k = 1
-            while 2 * k + (left - 1) * k <= len(pool):
-                k *= 2
-            out[c] = pool[:k]
-            used += pool[:k]
-            pool = pool[k:]
-    return out
+    pool = topo.engines(src, far[0])
+    k = 1
+    while 2 * k * len(far) <= len(pool):
+        k *= 2
+    out = {c: pool[k * n:k * n + k] for n, c in enumerate(far)}
+    used = pool[:k * len(far)]
+    for c in near:
+        out[c] = [e for e in topo.engines(src, c) if e not in used][:k]
+        used = used + out[c]
+    return {c: out[c] if many is True else out[c][many:many + 1] for c in out}
 
 
 def rank_program(g, core, T, topo):
@@ -104,32 +110,28 @@ def rank_program(g, core, T, topo):
     V, S, PE = g.vector, g.scalar, g.tensor
     known = {q: {} for q in Q}
     total = {}
-    recs = []
+    recs = {}
     ndma = [0]
 
     def span(reg):
         name, c0, c1 = reg
-        where, shape, dtp = SCRATCH[name]
+        where, shape, dtp = SCRATCH[name.split(".")[0]]
         if where != "sbuf":
             return (name, 0, 1 << 30)
         z = SIZE[dtp]
         return (name, c0 * z // 16 * 16, (c1 * z + 15) // 16 * 16)
 
-    def op(q, fn, reads, writes, dma=False):
+    def op(q, fn, reads, writes, dma=False, beside=()):
         rd = [span(x) for x in reads]
         wr = [span(x) for x in writes]
         needs = {}
-        for (q2, rd2, wr2, s2, v2, clock) in recs:
-            hit = False
-            for (n, a, b) in rd + wr:
-                ps = SCRATCH[n][0] == "psum"
-                if ps and q2 == q:
-                    continue
-                for (n2, a2, b2) in wr2 + (rd2 if (ps or (n, a, b) in wr) else []):
-                    if n2 == n and a < b2 and a2 < b:
-                        hit = True
-            if hit and needs.get(s2, (0, None))[0] < v2:
-                needs[s2] = (v2, clock)
+        for writing, regs in ((False, rd), (True, wr)):
+            for (n, a, b) in regs:
+                ps = n in SCRATCH and SCRATCH[n][0] == "psum"
+                for (q2, wrote, a2, b2, s2, v2, clock) in recs.get(n, []):
+                    if ((q2 != q if ps else (wrote or writing) and a < b2 and a2 < b) and s2 not in beside
+                            and needs.get(s2, (0, None))[0] < v2):
+                        needs[s2] = (v2, clock)
         for s2 in needs:
             v2 = needs[s2][0]
             if known[q].get(s2, 0) >= v2:
@@ -157,17 +159,17 @@ def rank_program(g, core, T, topo):
         total[sem] = val
         clock = dict(known[q])
         clock[sem] = val
-        recs.append((q, rd, wr, sem, val, clock))
+        for wrote, regs in ((False, rd), (True, wr)):
+            for (n, a, b) in regs:
+                recs.setdefault(n, []).append((q, wrote, a, b, sem, val, clock))
+        return sem
 
-    def dma(q, pairs, reads, writes):
-        op(q, lambda: [Q[q].dma_start(o, i) for (o, i) in pairs], reads, writes, True)
+    def dma(q, pairs, reads, writes, beside=()):
+        return op(q, lambda: [Q[q].dma_start(o, i) for (o, i) in pairs], reads, writes, True, beside)
 
-    plans = {c: deal_engines(c, cores, topo) for c in cores}
-    arrive = sum(len(plans[c][core]) for c in cores if c != core)
-
-    def exchange(pairs, reg, source, src_of, land, sem, q="y"):
-        dma(q, pairs, [reg], [(land, 0, 1), source])
-        def send():
+    def send(source, src_of, dst, land, sem, many):
+        plans = {c: deal_engines(c, cores, topo, many) for c in cores}
+        def fn():
             trs = []
             for k, c in enumerate(cores):
                 if c == core:
@@ -175,15 +177,24 @@ def rank_program(g, core, T, topo):
                 rid, pid, _ = topo.addr(c)
                 trs.append(RemoteDMATransfer(dst_ids=[DstId(rid=rid, pnc=pid)],
                                              dma_engine_mask=sum(1 << e for e in plans[core][c]),
-                                             remote_sem=T.sem[sem], src=src_of(k), dst=T[land][r]))
+                                             remote_sem=T.sem[sem], src=src_of(k), dst=dst))
             g.remote_dma_fused(trs, local_sem=T.sem.loc)
             total["loc"] = total.get("loc", 0) + sum(len(plans[core][c]) for c in plans[core])
-        op("g", send, [source], [])
-        total[sem] = arrive
-        recs.append(("far", [], [span((land, 0, 1))], sem, arrive, {sem: arrive}))
+        op("g", fn, [source], [])
+        total[sem] = sum(len(plans[c][core]) for c in cores if c != core)
+        for reg in land:
+            recs.setdefault(reg[0], []).append(("far", True) + span(reg)[1:] + (sem, total[sem], {sem: total[sem]}))
 
-    def spread(src, reg, land, sem):
-        exchange([(T[land][r], src)], reg, (land, 0, 1), lambda k: T[land][r], land, sem)
+    def exchange(pairs, reg, source, src_of, land, sem, q, many=True):
+        dma(q, pairs, [reg], [(land, 0, 1), source])
+        send(source, src_of, T[land][r], [(land, 0, 1)], sem, many)
+
+    def spread(src, reg, land, sem, staged):
+        if staged:
+            exchange([(T[land][r], src)], reg, (land, 0, 1), lambda k: T[land][r], land, sem, "y")
+        else:
+            dma("y", [(T[land][r], src)], [reg], [(land, 0, 1)])
+            send(reg, lambda k: src, T[land][r], [(land, 0, 1)], sem, True)
 
     def vts(dst, d0, d1, src, s0, s1, *ops):
         a = (ops[1], None, ops[0]) if len(ops) == 2 else (ops[1], ops[3], ops[0], ops[2])
@@ -205,9 +216,11 @@ def rank_program(g, core, T, topo):
 
     def gather(q, dst, d0, win, w0, w1, ofs, o0, o1, minus=None, other=None, how=A.min):
         n = 16 * (o1 - o0)
+        if n <= 0:
+            return
         src = T[win][:, w0:w1].indirect(T[ofs][:, o0:o1])
         out = T[dst][:, d0:d0 + n]
-        reads = [(win, w0, w1), (ofs, o0, o1)]
+        reads = [(win, w0, w1)] + [(n, o0, o1) for n in (["off.0", "off.1"] if ofs == "off" else [ofs])]
         if other:
             reads.append((other[0], other[1], other[1] + n))
             fn = lambda: V.tensor_tensor(out, src, T[other[0]][:, other[1]:other[1] + n], how)
@@ -221,100 +234,145 @@ def rank_program(g, core, T, topo):
             fn = lambda: S.activation(out, src, F.Copy)
         op(q, fn, reads, [(dst, d0, d0 + n)])
 
-    def shared(dst, d0, win, w0, w1, j):
-        c, n = 128 * j, SHARE[j]
-        gather("s", dst, d0, win, w0, w1, "lst", c, c + n)
-        gather("v", dst, d0 + 16 * n, win, w0, w1, "lst", c + n, c + 128)
+    work = []
 
-    def level(k, l, hooks, own=HELP):
+    def at(place):
+        for name, fn in work:
+            if PLAN[name] == place:
+                fn()
+
+    def by_list(q, j):
+        dst, d0, win, w1 = (("v2", 2048, "v1", 8192), ("xu", 2048, "v2", 6144), ("v3", 2048, "v2", 8192),
+                            ("xu", 2048, "v3", 6144))[j]
+        c0, c1 = (0, SHARE[j]) if q == "s" else (SHARE[j], 128)
+        gather(q, dst, d0 + 16 * c0, win, 2048, w1, "lst", 128 * j + c0, 128 * j + c1)
+        at("x%d%s" % (j, q))
+
+    def level(k, l, done):
         v, tb = "v%d" % k, "tb%d" % l
-        w0, w1, ofs, ob, oa = ((2048, 4096, "abu", 0, 128) if l == 0 else (2048, 6144, "abu", 256, 384) if k == 1
-                               else (0, 4096, "abx", 0, 128))
-        for n in range(len(CUTS) - 1):
-            c0, c1 = CUTS[n], CUTS[n + 1]
-            h = c1 - own if n == 0 else c1
-            gather("s", tb, 16 * c0, v, w0, w1, ofs, ob + c0, ob + h, 255.0)
-            if h < c1:
-                gather("v", tb, 16 * h, v, w0, w1, ofs, ob + h, ob + c1, 255.0)
-            for fn in hooks.get(("b", n), []):
-                fn()
-            gather("v", v, 4096 + 2048 * l + 16 * c0, v, w0, w1, ofs, oa + c0, oa + c1, None, (tb, 16 * c0))
-            for fn in hooks.get(("a", n), []):
-                fn()
+        w, w0, w1 = (v, 2048, 4096 + 2048 * l) if l == 0 or k == 1 else ("xu", 0, 4096)
+        ofs, ob, oa = "abu", 256 * l, 256 * l + 128
+        cuts = CUTS[2 * (k - 1) + l]
+        last = len(cuts) - 1
+        for n in range(last):
+            c0, c1 = cuts[n], cuts[n + 1]
+            h = 128 - HELP[2 * (k - 1) + l]
+            gather("s", tb, 16 * c0, w, w0, w1, ofs, ob + c0, ob + min(h, c1), 255.0)
+            if n == 0:
+                gather("v", tb, 16 * h, w, w0, w1, ofs, ob + h, ob + 128, 255.0)
+            at("b%d%d.%d" % (k, l, n))
+            o = 4096 + 2048 * l
+            gather("v", v, o + 16 * c0, w, w0, w1, ofs, oa + c0, oa + c1, None, (tb, 16 * c0))
+            if c0 // 16 < c1 // 16:
+                done(c0 // 16, c1 // 16)
+            at("a%d%d.%d" % (k, l, n))
 
-    def votes(k, l, who, gap=None):
+    def votes(k, l):
         v, vc = "v%d" % k, "vc%d" % l
         o = 4096 + 2048 * l
-        def pack(b, src, s0, first):
+        parts = [[t for t in range(3) if 128 * t < 48 * u + 48 and 48 * u < 128 * t + 128] for u in range(8)]
+        left = [2 * sum(t in p for p in parts) for t in range(3)]
+        whole = list(left)
+        def pack(src, s0, u0, u1):
             def fn():
-                PE.matmul(T["pd%d" % b][:, 0:256], T.wp[:, 16:144], T[src][:, s0:s0 + 256], first, False)
-                return PE.matmul(T["pd%d" % b][:, 0:256], T.wp[:, 10:138], T[src][:, s0 + 256:s0 + 512], False, not first)
-            op("t", fn, [("wp", 0, 160), (src, s0, s0 + 512)], [("pd%d" % b, 0, 256)])
-        def part(q, c0, c1):
-            gather(q, vc, 16 * c0, v, 2048, o + 16 * c1, "cdu", 128 * l + c0, 128 * l + c1, 0.0)
-        cut = SPLIT[2 * (k - 1) + l]
-        for b in range(2):
-            pack(b, v, o + 512 * b, True)
-            part("s", 32 * b, 32 * b + 32)
-            pack(b, vc, 512 * b, False)
-        part("s", 64, cut)
-        part("v", cut, 128)
-        for first in (True, False):
-            for b in (2, 3):
-                pack(b, v if first else vc, (o if first else 0) + 512 * b, first)
-        for b in range(4):
-            pd, a0 = "pd%d" % b, 256 * b
-            if b == 2 and gap:
-                gap()
-            if who[b] == "v":
-                vts("ad", a0, a0 + 256, pd, 0, 256, A.not_equal, 0.0)
+                for u in range(u0, u1):
+                    for t in parts[u]:
+                        left[t] -= 1
+                        c = 128 - 48 * u + 128 * t
+                        ins = PE.matmul(T["pd%d" % t][:, 0:256], T.wp[:, c:c + 128], T[src][:, s0 + 256 * u:s0 + 256 * u + 256],
+                                        left[t] + 1 == whole[t], left[t] == 0)
+                return ins
+            op("t", fn, [("wp", 0, 304), (src, s0 + 256 * u0, s0 + 256 * u1)],
+               [("pd%d" % t, 0, 256) for t in range(parts[u0][0], parts[u1 - 1][-1] + 1)])
+        def cands(q, u0, u1):
+            gather(q, vc, 256 * u0, v, 2048, o + 256 * u1, "cdu", 128 * l + 16 * u0, 128 * l + 16 * u1, 0.0)
+        def not_zero(t):
+            if who[t] == "v":
+                vts("ad", 256 * t, 256 * t + 256, "pd%d" % t, 0, 256, A.not_equal, 0.0)
             else:
-                act("ad", a0, pd, 256, F.Abs)
+                act("ad", 256 * t, "pd%d" % t, 256, F.Abs)
+        def add(t):
             def fn():
                 for m in range(2):
-                    c = WM + 15 - 4 * b - m
-                    ins = PE.matmul(T.pv[:, 0:128], T.ww[:, c:c + 128], T.ad[:, a0 + 128 * m:a0 + 128 * m + 128],
-                                    b == 0 and m == 0, b == 3 and m == 1)
+                    c = WS + 144 * t + 15 - m
+                    ins = PE.matmul(T.pv[:, 0:128], T.ww[:, c:c + 128], T.ad[:, 256 * t + 128 * m:256 * t + 128 * m + 128],
+                                    t + m == 0, t + m == 3)
                 return ins
-            op("t", fn, [("ww", WM, WM + 144), ("ad", a0, a0 + 256)], [("pv", 0, 128)])
+            op("t", fn, [("ww", WS, WS + 432), ("ad", 256 * t, 256 * t + 256)], [("pv", 0, 128)])
+        (a, b, c), who = PACK[2 * (k - 1) + l]
+        if not who:
+            level(k, l, lambda u0, u1: None)
+            return
+        level(k, l, lambda u0, u1: pack(v, o, u0, u1))
+        cands("s", 0, a)
+        pack(vc, 0, 0, a)
+        cands("s", a, b)
+        at("p%d%d" % (k, l))
+        cands("v", b, c)
+        for u0, u1 in sorted([(a, b), (b, c)], key=lambda x: x[1] - x[0] + (a - 2 if x[0] == a else 0)):
+            if u0 < u1:
+                pack(vc, 0, u0, u1)
+        at("c%d%d.0" % (k, l))
+        cands("v", c, 8)
+        pack(vc, 0, c, 8)
+        work[0:3] = [("sum%d%d.%d" % (k, l, t), lambda t=t: [not_zero(t), add(t)]) for t in range(3)]
+        at("e%d%d" % (k, l))
 
-    def send_votes(k, l, q):
+    def unequal(i0, i1):
+        if i0 == i1:
+            return
+        gather("v", "vc1", 128 * i0, "v2", 2048, 8192, "cdu", 128 + 8 * i0, 128 + 8 * i1, None, ("tw", 128 * i0), A.not_equal)
+        def fn():
+            for i in range(i0, i1):
+                ins = PE.matmul(T.px1[:, 0:128], T.ww[:, WE + 15 - i:WE + 143 - i], T.vc1[:, 128 * i:128 * i + 128],
+                                i == 0, i == 15)
+            return ins
+        op("t", fn, [("ww", WE, WE + 144), ("vc1", 128 * i0, 128 * i1)], [("px1", 0, 128)])
+
+    def send_votes(k, l, q, dq):
         ph = 2 * (k - 1) + l
         la, sg = "la%d" % ph, "sg%d" % ph
         c0 = 128 * ph
+        pv = "px1" if ph == 3 else "pv"
         if q == "v":
-            vcp("cnt", c0, "pv", 0, 128)
+            vcp("cnt", c0, pv, 0, 128)
         else:
-            act("cnt", c0, "pv", 128, F.Copy)
+            act("cnt", c0, pv, 128, F.Copy)
         exchange([(T[sg][:], T.cnt[:, c0:c0 + 128]), (T[la][r], T.cnt[16 * r:16 * r + 16, c0:c0 + 128])],
-                 ("cnt", c0, c0 + 128), (sg, 0, 1), lambda j: T[sg][j], la, "aa%d" % ph, "y" if q == "v" else "s")
+                 ("cnt", c0, c0 + 128), (sg, 0, 1), lambda j: T[sg][j], la, "aa%d" % ph, dq, ph if ph < 2 else True)
 
     def window(k):
         return ("v1", 2048) if k == 3 else ("win", 0)
 
-    def load_counts(k, l):
+    def load_counts(k, l, qs="y"):
         la = "la%d" % (2 * (k - 1) + l)
         w, b = window(k)
         c0 = b + 16 + 2048 * l
-        dma("y", [(T[w][16 * j:16 * j + 8, c0:c0 + 2048], T[la][:]) for j in range(8)], [(la, 0, 1)], [(w, c0, c0 + 2048)])
+        mine = []
+        for n, q in enumerate(qs):
+            mine.append(dma(q, [(T[w][16 * j:16 * j + 8, c0:c0 + 2048], T[la][:]) for j in range(n, 8, len(qs))],
+                            [(la, 0, 1)], [(w, c0, c0 + 2048)], mine))
 
     def load_cands(k):
         w, b = window(k)
         dma("y", [(T[w][16 * j + 8:16 * j + 10, b + 16:b + 4112], T.ctab[:]) for j in range(8)],
             [("ctab", 0, 1)], [(w, b + 16, b + 4112)])
 
-    def pick(ps, p0, wt, src, s0, s1):
-        n = (s1 - s0) // 16
+    def pick(ps, p0, wt, src, s0, s1, step=1):
+        n = ((s1 - s0) // 16 - 1) * step + 1
         def fn():
             for i in range(16):
                 c = wt + 15 - i
-                ins = PE.matmul(T[ps][:, p0:p0 + n], T.ww[:, c:c + 128], T[src][:, s0 + i:s1:16], i == 0, i == 15)
+                ins = PE.matmul(T[ps][:, p0:p0 + n:step], T.ww[:, c:c + 128], T[src][:, s0 + i:s1:16], i == 0, i == 15)
             return ins
         op("t", fn, [("ww", wt, wt + 144), (src, s0, s1)], [(ps, p0, p0 + n)])
 
-    def offsets(slot, a, b):
-        c = 32 * slot
-        vts("off", c + a, c + b, "stt", c + a, c + b, A.subtract, 2032.0, A.max, 15.0)
+    def track(slot, lane, src, reg):
+        d, o = 64 * slot + 3 * lane, 32 * slot + lane
+        for out, where in ([(T.off[:, o:o + 31:2], ("off.%d" % lane, 32 * slot, 32 * slot + 32))]
+                           + [(T.oa[:, 16 * slot:16 * slot + 16], ("oa", 16 * slot, 16 * slot + 16))] * lane):
+            op("v", lambda: V.tensor_scalar(out, src, 2032.0, 15.0, A.subtract, A.max), [reg], [where])
+        op("v", lambda: V.tensor_copy(T.dd[:, d:d + 61:4], src), [reg], [("dd.%d" % lane, 64 * slot, 64 * slot + 64)])
 
     def look(qs, slot, k, l):
         w, b = window(k)
@@ -322,37 +380,38 @@ def rank_program(g, core, T, topo):
         for n, q in enumerate(qs):
             o = 32 * slot + per * n
             gather(q, "gq%d" % l, 16 * per * n, w, b, b + 16 + 2048 * (l + 1), "off", o, o + per)
-        pick("px%d" % l, 0, WC, "gq%d" % l, 0, 512)
+        pick("px%d" % l, 257, WC, "gq%d" % l, 0, 512, 2)
 
-    def choose(slot, nxt, l):
-        px = "px%d" % l
-        c = 32 * slot
-        vtt("sm", 0, 16, px, 16, "stt", c + 16, A.min)
-        vtt("sm", 16, 16, px, 0, "stt", c + 16, A.subtract)
-        vtt("sm", 32, 16, "sm", 0, "sm", 16, A.add)
-        vtt("stt", 32 * nxt, 16, "sm", 32, "stt", c, A.min)
+    def choose(slot, l):
+        px, c, s = "px%d" % l, 64 * slot, 64 * l
+        op("v", lambda: V.tensor_tensor_scan(T.sm[:, s:s + 64], T[px][:, 256:320], T.dd[:, c:c + 64], 0.0, A.subtract, A.min),
+           [(px, 0, 1), ("dd.0", c, c + 64), ("dd.1", c, c + 64), ("dd.3", 0, 384)], [("sm", s, s + 64)])
+        return T.sm[:, s + 3:s + 64:4], ("sm", s, s + 64)
 
-    def share_list(slot, j):
-        vcp("su", 16 * j, "stt", 32 * slot, 16)
-        spread(T.su[:, 16 * j:16 * j + 16], ("su", 16 * j, 16 * j + 16), "lb%d" % j, "ab%d" % j)
-        offsets(slot, 0, 16)
+    def share_list(slot, l, j, nxt=None):
+        ln, c = "ln%d" % j, 16 * r
+        new, reg = choose(slot, l)
+        op("v", lambda: V.tensor_copy(T[ln][:, c:c + 16], new), [reg], [(ln, c, c + 16)])
+        send((ln, c, c + 16), lambda k: T[ln][:, c:c + 16], T[ln][:, c:c + 16], [(ln, 0, c), (ln, c + 16, 128)],
+             "ab%d" % j, True)
+        if nxt:
+            track(nxt, 1, new, reg)
 
     def load_list(j):
-        c = 128 * (j + 1)
-        dma("y", [(T.lst[:, c:c + 128], T["lb%d" % j][:])], [("lb%d" % j, 0, 1)], [("lst", c, c + 128)])
+        ln = "ln%d" % j
+        op("t", lambda: PE.matmul(T.pl[:, 0:128], T[ln][:, 0:128], T.eye[:, 0:128], True, True),
+           [(ln, 0, 128), ("eye", 0, 128)], [("pl", 0, 128)])
+        vcp("lst", 128 * (j + 1), "pl", 0, 128)
 
-    def ahead_gather(slot, k, l):
-        w, b = window(k)
-        gather("s", "gp", 0, w, b, b + 16 + 2048 * (l + 1), "off", 32 * slot, 32 * slot + 16)
+    def ahead_gather(slot, w, b, l):
+        gather("s", "gp", 0, w, b, b + 16 + 2048 * (l + 1), "oa", 16 * slot, 16 * slot + 16)
         pick("pp", 0, WF, "gp", 0, 256)
 
     def ahead_finish(slot):
-        c = 32 * slot
-        vtt("stt", c + 16, 16, "pp", 0, "stt", c, A.min)
-        offsets(slot, 16, 32)
+        track(slot, 0, T.pp[:, 0:16], ("pp", 0, 16))
 
-    def store_values(c0, c1):
-        dma("y", [(T.yv[:, c0:c1], T.v3[:, 2048 + c0:2048 + c1])], [("v3", 2048 + c0, 2048 + c1)], [])
+    def store_values(c0, c1, q="s"):
+        dma(q, [(T.yv[:, c0:c1], T.v3[:, 2048 + c0:2048 + c1])], [("v3", 2048 + c0, 2048 + c1)], [])
 
     def count_up(name, c0, n, step, base, cm):
         kw = {} if SCRATCH[name][2] == "int32" else {"allow_small_or_imprecise_dtypes": True}
@@ -362,39 +421,57 @@ def rank_program(g, core, T, topo):
         op("g", lambda: g.affine_select(T[name][:, c0:c0 + n], T[name][:, s0:s0 + n], pattern, cmp, other, base, cm),
            [(name, s0, s0 + n)], [(name, c0, c0 + n)])
 
-    R0, R1, R2, T0, T1, T2, R3, T3 = range(8)
+    def band(c, s, lo, hi):
+        op("g", lambda: g.affine_select(T.bnd[:, 8:16], T.bnd[:, s:s + 8], [[-16, 8]], A.is_ge, 0.0, -lo, 1),
+           [("bnd", s, s + 8)], [("bnd", 8, 16)])
+        op("g", lambda: g.affine_select(T.ww[:, c:c + 113:16], T.bnd[:, 8:16], [[16, 8]], A.is_ge, 0.0, hi, -1),
+           [("bnd", 8, 16)], [("ww", c, c + 113)])
+
+    R0, T0, R1, T1, R2, T2 = range(6)
 
     dma("y", [(T.ab[:, 0:128], T.fb[:, 0:128])], [], [("ab", 0, 128)])
     dma("s", [(T.ab[:, 128:256], T.fa[:, 0:128])], [], [("ab", 128, 256)])
     dma("s", [(T.v1[:, 2048:4096], T.x[:])], [], [("v1", 2048, 4096)])
-    dma("y", [(T.cdi[:], T.cd[:])], [], [("cdi", 0, 256)])
-    dma("y", [(T.ab[:, 256:384], T.fb[:, 128:256]), (T.ab[:, 384:512], T.fa[:, 128:256])], [], [("ab", 256, 512)])
-    dma("y", [(T.tpi[:], T.tp[:]), (T.own[:, 0:16], T.cd[16 * r:16 * r + 16, 0:128]),
-              (T.own[:, 16:32], T.tp[16 * r:16 * r + 16, 0:128])], [], [("tpi", 0, 128), ("own", 0, 32)])
-    fill("win", 16, 4112, 0.0)
-    fill("win", 0, 16, BIG / 2)
-    fill("ww", 0, 576, 0.0)
-    count_up("sel", 0, 16, 0, 1, 0)
-    count_up("bnd", 32, 8, 0, 1, 0)
-    count_up("bnd", 0, 8, 0, BIG, 0)
-    keep("sel", 0, 0, 16, [[-1, 16]], A.is_equal, 0.0, -16 * r, 1)
-    keep("bnd", 0, 0, 8, [[16, 8]], A.is_ge, 1.0, 7, -1)
-    for c, lo in ((8, 8), (16, 0), (24, 6), (40, 0), (0, 0)):
-        keep("bnd", c, 32 if c else 0, 8, [[-16, 8]], A.is_ge, 0.0, -lo, 1)
-    for c, hi in ((8, 9), (16, 5), (24, 15), (40, 15), (0, 9)):
-        keep("bnd", c, c, 8, [[16, 8]], A.is_ge, 0.0, hi, -1)
-    count_up("wp", 0, 16, 0, 0, 0)
-    count_up("wp", 16, 144, 0, 65536, 0)
-    keep("wp", 16, 16, 144, [[-16, 9], [-3, 16]], A.is_ge, 256.0, -2, 1)
-    keep("wp", 16, 16, 144, [[-16, 9], [-3, 16]], A.is_ge, 1.0, -1, 1)
-    keep("wp", 16, 16, 144, [[-16, 9], [-3, 16]], A.is_ge, 0.0, 0, 1)
-    keep("wp", 16, 16, 144, [[16, 9], [3, 16]], A.is_ge, 0.0, 2, -1)
-    keep("wp", 16, 16, 144, [[16, 9], [0, 16]], A.is_ge, 0.0, 15, -1)
-    count_up("ti", 0, 16, 16, 2048, 256)
-    count_up("pi", 0, 4, 0, 0, 1)
+    dma("y", [(T.cdi[:], T.cd[:])], [("ab", 0, 256)], [("cdi", 0, 256)])
+    dma("y", [(T.ab[:, 256:384], T.fb[:, 128:256]), (T.ab[:, 384:512], T.fa[:, 128:256])], [("v1", 2048, 4096)],
+        [("ab", 256, 512)])
+    dma("y", [(T.tpi[:], T.tp[:])], [], [("tpi", 0, 128)])
+    count_up("w1", 0, 16, 0, 0, 1)
+    count_up("stt", 0, 16, 1, 2048, 16)
+    fill("wp", 0, 304, 0.0)
+    fill("ww", 0, 864, 0.0)
+    op("v", lambda: V.memset(T.dd[:, 1:384:4], 0.0), [], [("dd.2", 0, 384)])
+    op("v", lambda: V.memset(T.dd[:, 2:384:4], BIG), [], [("dd.3", 0, 384)])
+    for px in ("px0", "px1"):
+        op("v", lambda: V.memset(T[px][:, 256:320:4], 2 * BIG), [], [(px, 0, 1)])
+        op("v", lambda: V.memset(T[px][:, 258:320:4], 0.0), [], [(px, 0, 1)])
+    vts("w1", 16, 32, "w1", 0, 16, A.bitwise_and, 8)
+    track(R0, 1, T.stt[:, 0:16], ("stt", 0, 16))
+    vts("win", 0, 16, "w1", 16, 32, A.is_equal, 0.0)
+    fill("win", 16, 2064, 0.0)
     vcp("abu", 0, "ab", 0, 256)
-    for c, s in ((WC + 15, 0), (WF + 15, 8), (WM + 15, 16), (WM + 17, 24), (WE + 15, 40)):
-        vcp("ww", c, "bnd", s, 8, 16)
+    fill("win", 2064, 4112, 0.0)
+    count_up("wp", 128, 48, 0, 65536, 0)
+    keep("wp", 128, 128, 48, [[-16, 8], [-3, 6]], A.is_ge, 256.0, -2, 1)
+    keep("wp", 128, 128, 48, [[-16, 8], [-3, 6]], A.is_ge, 1.0, -1, 1)
+    keep("wp", 128, 128, 48, [[-16, 8], [-3, 6]], A.is_ge, 0.0, 0, 1)
+    keep("wp", 128, 128, 48, [[16, 8], [3, 6]], A.is_ge, 0.0, 2, -1)
+    keep("wp", 128, 128, 48, [[16, 8], [0, 6]], A.is_ge, 0.0, 15, -1)
+    count_up("bnd", 32, 64, 0, 1, 0)
+    for t in range(3):
+        c = WS + 144 * t + 15
+        keep("bnd", 96, 32, 64, [[-6, 8], [-48, 8]], A.is_ge, 0.0, 128 * t, 1)
+        op("g", lambda: g.affine_select(T.ww[:, c:c + 127:2], T.bnd[:, 96:160], [[6, 8], [48, 8]], A.is_ge, 0.0,
+                                        5 - 128 * t, -1), [("bnd", 96, 160)], [("ww", c, c + 127)])
+    count_up("sel", 0, 16, 0, 1, 0)
+    keep("sel", 0, 0, 16, [[-1, 16]], A.is_equal, 0.0, -16 * r, 1)
+    band(WF + 15, 32, 8, 9)
+    band(WE + 15, 32, 0, 15)
+    count_up("bnd", 0, 8, 0, BIG, 0)
+    keep("bnd", 0, 0, 8, [[16, 8]], A.is_ge, 1.0, 7, -1)
+    band(WC + 15, 0, 0, 9)
+    count_up("eye", 0, 128, 0, 1, 0)
+    keep("eye", 0, 0, 128, [[-1, 128]], A.is_equal, 0.0, 0, 1)
 
     def turn():
         PE.matmul(T.pp[:, 0:16], T.cdf[:, 0:256:2], T.sel[:, 0:16], True, True)
@@ -403,118 +480,122 @@ def rank_program(g, core, T, topo):
         vcp("chl", 0, "pp", 0, 32)
         vtt("chl", 32, 32, "pp", 0, "chl", 0, A.subtract)
         dma("y", [(T.ctab[0], T.chl[:, 0:32]), (T.ctab[1], T.chl[:, 32:64])], [("chl", 0, 64)], [("ctab", 0, 1)])
-        load_cands(1)
+    def turn_lists():
+        PE.matmul(T.pl[:, 0:16], T.cdf[:, 0:128], T.sel[:, 0:16], True, True)
+        return PE.matmul(T.pl[:, 16:32], T.tpf[:, 0:128], T.sel[:, 0:16], True, True)
+    def first_states():
+        track(R0, 0, T.pl[:, 0:16], ("pl", 0, 16))
+        track(T0, 1, T.pl[:, 16:32], ("pl", 0, 16))
+    def last_list(ps, out, c):
+        vtt("abf", 256 + c, 128, ps, 0, "abf", 256 + c, A.min)
+        dma("y" if c == 0 else "s", [(out[:, 128:256], T.abf[:, 256 + c:384 + c])], [("abf", 256 + c, 384 + c)], [])
+    def share_last():
+        new, reg = choose(R2, 0)
+        op("v", lambda: V.tensor_copy(T.sb[:, 0:32:2], new), [reg], [("sb", 0, 32)])
+        op("v", lambda: V.tensor_tensor(T.sb[:, 1:32:2], new, T.sb[:, 0:32:2], A.subtract),
+           [reg, ("sb", 0, 32)], [("sb", 0, 32)])
+        spread(T.sb[:, 0:32], ("sb", 0, 32), "lb3", "ab3", STAGE[0])
+    def share_taps():
+        new, reg = choose(T2, 1)
+        op("v", lambda: V.tensor_copy(T.stt[:, 16:32], new), [reg], [("stt", 16, 32)])
+        spread(T.stt[:, 16:32], ("stt", 16, 32), "lb4", "ab4", STAGE[1])
+    def inputs_again(k, q):
+        dma(q, [(T.xu[:, 0:2048], T["v%d" % k][:, 2048:4096])], [("v%d" % k, 2048, 4096)], [("xu", 0, 2048)])
 
-    level(1, 0, {("a", 2): [lambda: vcp("cdu", 0, "cdi", 0, 256)]})
-    vcp("abu", 256, "ab", 256, 128)
-    votes(1, 0, "vvvv", lambda: vcp("abu", 384, "ab", 384, 128))
-    vcp("cdf", 0, "cdi", 0, 256)
-    send_votes(1, 0, "v")
-    op("t", turn, [("cdf", 0, 256), ("sel", 0, 16)], [("pp", 0, 32)])
-    level(1, 1, {("a", 0): [split]}, 0)
-    load_counts(1, 0)
-    vcp("lst", 0, "tpi", 0, 128)
-    votes(1, 1, "vvvv")
-    vcp("stt", 32 * T0, "own", 16, 16)
-    shared("v2", 2048, "v1", 2048, 8192, 0)
-    send_votes(1, 1, "v")
-    fill("v1", 2048, 2064, BIG / 2)
-    load_cands(3)
-    vts("pj", 0, 4, "pi", 0, 4, A.arith_shift_right, 3)
-    vcp("stt", 32 * R0 + 16, "own", 0, 16)
-    vts("pk", 0, 4, "pj", 0, 4, A.mult, -2047.0)
-    vts("w1", 0, 256, "ab", 256, 512, A.add, 2048.0)
-    op("v", lambda: V.tensor_scalar(T.stt[:, 0:16], T.ti[:, 0:16], T.pk[:, 0:1], None, A.add),
-       [("ti", 0, 16), ("pk", 0, 4)], [("stt", 0, 16)])
+    cut = 4096 + 16 * CUTS[5][2]
+    steps = [
+        ("cand0", lambda: vcp("cdu", 0, "cdi", 0, 128)),
+        ("fanb1", lambda: vcp("abu", 256, "ab", 256, 128)),
+        ("candf", lambda: vcp("cdf", 0, "cdi", 0, 256)),
+        ("send10", lambda: send_votes(1, 0, LQ[4], DQ[0])),
+        ("turn", lambda: op("t", turn, [("cdf", 0, 256), ("sel", 0, 16)], [("pp", 0, 32)])),
+        ("fana1", lambda: vcp("abu", 384, "ab", 384, 128)),
+        ("table", lambda: [split(), load_cands(1)]),
+        ("tapf", lambda: [vcp("tpf", 0, "tpi", 0, 128),
+                          op("t", turn_lists, [("cdf", 0, 128), ("tpf", 0, 128), ("sel", 0, 16)], [("pl", 0, 32)])]),
+        ("cand1", lambda: vcp("cdu", 128, "cdi", 128, 128)),
+        ("first", first_states),
+        ("taps0", lambda: vcp("lst", 0, "tpi", 0, 128)),
+        ("load10", lambda: load_counts(1, 0)),
+        ("send11", lambda: send_votes(1, 1, LQ[5], DQ[1])),
+        ("table3", lambda: [vcp("v1", 2048, "win", 0, 16), load_cands(3)]),
+        ("lookR0", lambda: look(LQ[0], R0, 1, 0)),
+        ("shareR1", lambda: share_list(R0, 0, 0, R1)),
+        ("load11", lambda: load_counts(1, 1)),
+        ("aheadT0", lambda: ahead_gather(T0, "v1", 2048, 1)),
+        ("candT0", lambda: ahead_finish(T0)),
+        ("again2", lambda: inputs_again(2, DQ[9])),
+        ("send20", lambda: send_votes(2, 0, LQ[6], DQ[2])),
+        ("listR1", lambda: load_list(0)),
+        ("aheadR1", lambda: ahead_gather(R1, "v1", 2048, 0)),
+        ("lookT0", lambda: look(LQ[1], T0, 1, 1)),
+        ("candR1", lambda: ahead_finish(R1)),
+        ("shareT1", lambda: share_list(T0, 1, 1)),
+        ("load20", lambda: load_counts(2, 0)),
+        ("lookR1", lambda: look(LQ[7], R1, 2, 0)),
+        ("listT1", lambda: load_list(1)),
+        ("shareR2", lambda: share_list(R1, 0, 2, R2)),
+        ("store0", lambda: store_values(0, 2048)),
+        ("flatT1", lambda: dma("y", [(T.su[:, 0:16], T.lst[16 * r:16 * r + 16, 256:384])], [("lst", 256, 384)],
+                               [("su", 0, 16)])),
+        ("again3", lambda: inputs_again(3, DQ[10])),
+        ("twin", lambda: dma("y", [(T.tw[:], T.v2[:, 6144:8192])], [("v2", 6144, 8192)], [("tw", 0, 2048)])),
+        ("late0", lambda: unequal(0, LATE[0])),
+        ("late1", lambda: unequal(LATE[0], LATE[1])),
+        ("late2", lambda: unequal(LATE[1], LATE[2])),
+        ("late3", lambda: unequal(LATE[2], 16)),
+        ("send21", lambda: send_votes(2, 1, LQ[2], DQ[3])),
+        ("aheadR2", lambda: ahead_gather(R2, "v1", 2048, 0)),
+        ("listR2", lambda: load_list(2)),
+        ("store1", lambda: store_values(2048, 4096)),
+        ("candR2", lambda: ahead_finish(R2)),
+        ("send30", lambda: send_votes(3, 0, LQ[8], DQ[4])),
+        ("load21", lambda: load_counts(2, 1)),
+        ("load30", lambda: load_counts(3, 0)),
+        ("store2", lambda: store_values(4096, cut)),
+        ("send31", lambda: send_votes(3, 1, LQ[3], DQ[5])),
+        ("lookR2", lambda: look(LQ[9], R2, 3, 0)),
+        ("stateT1", lambda: track(T1, 1, T.su[:, 0:16], ("su", 0, 16))),
+        ("aheadT1", lambda: ahead_gather(T1, "win", 0, 1)),
+        ("shareR3", share_last),
+        ("fin0", lambda: vts("w1", 0, 256, "ab", 256, 512, A.subtract, 2040.0, A.max, 0.0)),
+        ("candT1", lambda: ahead_finish(T1)),
+        ("lookT1", lambda: look(LQ[10], T1, 2, 1)),
+        ("store3", lambda: store_values(cut, 6144, DQ[6])),
+        ("fin1", lambda: [vts("abz", 0, 256, "w1", 0, 256, A.mult, 2.0), fill("v2", 2032, 2048, BIG / 2)]),
+        ("stateT2", lambda: track(T2, 1, *choose(T1, 1))),
+        ("aheadT2", lambda: ahead_gather(T2, "win", 0, 1)),
+        ("load31", lambda: load_counts(3, 1, DQ[7])),
+        ("fin2", lambda: vcp("abf", 0, "ab", 0, 256)),
+        ("candT2", lambda: ahead_finish(T2)),
+        ("rowsR3", lambda: dma(DQ[8], [(T.v2[8:128:16, 2048:6144], T.lb3[:]), (T.v2[9:128:16, 2047:6143], T.lb3[:])],
+                               [("lb3", 0, 1)], [("v2", 2047, 6144)])),
+        ("lookT2", lambda: look("vs", T2, 3, 1)),
+        ("fin3", lambda: vcp("abf", 256, "ab", 256, 256)),
+        ("shareT3", share_taps),
+        ("out0", lambda: dma("y", [(T.yb[:, 0:128], T.abf[:, 0:128]), (T.ya[:, 0:128], T.abf[:, 128:256])],
+                             [("abf", 0, 256)], [])),
+    ]
+    work.extend(steps[0:3] + steps)
+    work[0:3] = [("sum10.0", None)] * 3
 
-    offsets(R0, 0, 32)
-    offsets(T0, 0, 16)
-    level(2, 0, {("b", LOOK): [lambda: look("vs", R0, 1, 0)],
-                 ("a", LOOK + 1): [lambda: choose(R0, R1, 0), lambda: share_list(R1, 0)]}, 0)
-    load_counts(1, 1)
-    ahead_gather(T0, 3, 1)
-    votes(2, 0, "svvs", lambda: ahead_finish(T0))
-    vts("aby", 0, 256, "w1", 0, 256, A.bitwise_and, 4095)
-    load_list(0)
-    send_votes(2, 0, "s")
-    look("v", T0, 1, 1)
-    ahead_gather(R1, 3, 0)
-    vcp("abx", 0, "aby", 0, 256)
-    choose(T0, T1, 1)
-    share_list(T1, 1)
-    load_counts(2, 0)
-    shared("v2", 0, "v2", 2048, 6144, 1)
-    load_list(1)
-    level(2, 1, {("a", 0): [lambda: ahead_finish(R1)], ("b", 4): [lambda: look("vs", R1, 2, 0)]})
-    choose(R1, R2, 0)
-    share_list(R2, 2)
-
-    shared("v3", 2048, "v2", 2048, 8192, 2)
-    dma("y", [(T.tw[:], T.v2[:, 6144:8192])], [("v2", 6144, 8192)], [("tw", 0, 2048)])
-    load_list(2)
-    store_values(0, 2048)
-    level(3, 0, {})
-    ahead_gather(R2, 3, 0)
-    votes(3, 0, "ssss")
-    send_votes(3, 0, "s")
-    store_values(2048, 4096)
-    gather("v", "vc1", 0, "v2", 2048, 8192, "cdu", 128, 256, None, ("tw", 0), A.not_equal)
-    ahead_finish(R2)
-    shared("v3", 0, "v3", 2048, 6144, 3)
-    def plain():
-        for i in range(16):
-            c = WE + 15 - i
-            ins = PE.matmul(T.pv[:, 0:128], T.ww[:, c:c + 128], T.vc1[:, 128 * i:128 * i + 128], i == 0, i == 15)
-        return ins
-    op("t", plain, [("ww", WE, WE + 144), ("vc1", 0, 2048)], [("pv", 0, 128)])
-    level(3, 1, {("a", 0): [lambda: send_votes(2, 1, "v")], ("a", 1): [lambda: load_counts(3, 0)]})
-    ahead_gather(T1, 2, 1)
-    store_values(4096, 6144)
-    load_counts(2, 1)
-    votes(3, 1, "svvs", lambda: ahead_finish(T1))
-    send_votes(3, 1, "s")
-
-    look("v", R2, 3, 0)
-    choose(R2, R3, 0)
-    c = 32 * R3
-    vcp("sb", 0, "stt", c, 16, 2)
-    op("v", lambda: V.tensor_tensor(T.sb[:, 1:32:2], T.stt[:, c:c + 16], T.sb[:, 0:32:2], A.subtract),
-       [("stt", c, c + 16), ("sb", 0, 32)], [("sb", 0, 32)])
-    spread(T.sb[:, 0:32], ("sb", 0, 32), "lb3", "ab3")
-    look("s", T1, 2, 1)
-    fill("v2", 6144, 6160, BIG / 2)
-    vts("w1", 0, 256, "aby", 0, 256, A.bitwise_and, 15)
-    vts("w3", 0, 256, "aby", 0, 256, A.is_ge, 2048.0, A.mult, 65536.0)
-    vts("w2", 0, 256, "w1", 0, 256, A.mult, 2047.0)
-    choose(T1, T2, 1)
-    offsets(T2, 0, 16)
-    ahead_gather(T2, 2, 1)
-    vtt("w3", 0, 256, "w3", 0, "aby", 0, A.add)
-    vcp("abf", 0, "ab", 0, 512)
-    ahead_finish(T2)
-    vtt("w3", 0, 256, "w3", 0, "w2", 0, A.add)
-    vts("abz", 0, 256, "w3", 0, 256, A.mult, 0.125, A.min, 4096.0)
-    load_counts(3, 1)
-    dma("s", [(T.v2[8:128:16, 2048:6144], T.lb3[:]), (T.v2[9:128:16, 2047:6143], T.lb3[:])], [("lb3", 0, 1)],
-        [("v2", 2047, 6144)])
-    look("vs", T2, 3, 1)
-    choose(T2, T3, 1)
-    c3 = 32 * T3
-    dma("y", [(T.yb[:, 0:128], T.abf[:, 0:128]), (T.ya[:, 0:128], T.abf[:, 128:256])], [("abf", 0, 256)], [])
-    spread(T.stt[:, c3:c3 + 16], ("stt", c3, c3 + 16), "lb4", "ab4")
-    gather("s", "tb1", 0, "v2", 2048, 6160, "abz", 0, 64)
-    gather("v", "tb0", 1024, "v2", 2048, 6160, "abz", 192, 256)
-    gather("s", "tb1", 1024, "v2", 2048, 6160, "abz", 64, 128)
-    gather("v", "tb0", 16 * LAST, "v2", 2048, 6160, "abz", 128 + LAST, 192)
-    gather("s", "tb0", 0, "v2", 2048, 6160, "abz", 128, 128 + LAST)
-    pick("pv", 0, WF, "tb1", 0, 1024)
-    pick("px0", 64, WF, "tb0", 1024, 2048)
-    pick("pv", 64, WF, "tb1", 1024, 2048)
-    pick("px0", 0, WF, "tb0", 0, 1024)
-    vtt("abf", 256, 128, "pv", 0, "abf", 256, A.min)
-    dma("s", [(T.yb[:, 128:256], T.abf[:, 256:384])], [("abf", 256, 384)], [])
-    vtt("abf", 384, 128, "px0", 0, "abf", 384, A.min)
-    dma("s", [(T.ya[:, 128:256], T.abf[:, 384:512])], [("abf", 384, 512)], [])
+    for k in (1, 2, 3):
+        for l in (0, 1):
+            if k > 1:
+                by_list("s", 2 * (k - 2) + l)
+                by_list("v", 2 * (k - 2) + l)
+            votes(k, l)
+    for n in range(8):
+        at("end%d" % n)
+    for tb, ps, c in (("tb1", "pd0", 0), ("tb0", "pd1", 128)):
+        for h in (0, 64):
+            gather("s", tb, 16 * h, "v2", 2032, 6144, "abz", c + h, c + h + 32)
+            gather("v", tb, 16 * h + 512, "v2", 2032, 6144, "abz", c + h + 32, c + h + 64)
+            pick(ps, h, WF, tb, 16 * h, 16 * h + 1024)
+            at("f%d" % ((c + h) // 64))
+            if c and not h:
+                last_list("pd0", T.yb, 0)
+    last_list("pd1", T.ya, 128)
     dma("y", [(T.yt[:], T.lb4[:])], [("lb4", 0, 1)], [])
     for s in total:
         if known["g"].get(s, 0) < total[s]:

from concourse.bass import DstId, RemoteDMATransfer
from concourse.mybir import AluOpType, ActivationFunctionType

BIG = 8192
CUTS = [[0, 32, 64, 96, 128], [0, 32, 64, 96, 128], [0, 32, 64, 96, 128], [0, 28, 64, 100, 128], [0, 32, 64, 96, 128],
        [0, 20, 44, 68, 96, 128]]
HELP = [22, 4, 8, 16, 22, 26]
PACK = [((4, 6, 6), "vvs"), ((4, 4, 6), "vvv"), ((3, 5, 6), "svv"), ((3, 4, 6), ""), ((3, 7, 7), "sss"),
        ((4, 6, 7), "vvv")]
SHARE = [88, 72, 64, 84]
STAGE = [True, False]
LATE = [3, 5, 6]
DQ = ["y", "y", "y", "y", "y", "y", "y", "ys", "y", "y", "s"]
LQ = ["vs", "s", "v", "v", "v", "s", "v", "s", "v", "s", "s"]
PLACES = {
    "b10.0": "cand0 candf", "a10.2": "turn", "a10.3": "fanb1 fana1 taps0", "c10.0": "cand1", "e10": "sum10.0",
    "b11.0": "sum10.1 sum10.2 tapf", "b11.1": "send10 table", "x0v": "sum11.0 sum11.1 sum11.2 first table3",
    "b20.0": "load10", "a20.0": "send11 again2", "b20.1": "load11", "b20.2": "lookR0", "a20.2": "shareR1",
    "b20.3": "aheadT0", "c20.0": "candT0", "e20": "sum20.0 sum20.1 sum20.2 send20 listR1 lookT0", "x1s": "shareT1",
    "x1v": "aheadR1", "b21.0": "candR1", "a21.1": "load20", "b21.3": "listT1", "a21.3": "lookR1", "x2v": "shareR2",
    "b30.2": "aheadR2", "b30.3": "again3 twin", "a30.3": "store0", "p30": "late0 late1 late2 listR2",
    "c30.0": "store1", "e30": "sum30.0 sum30.1 sum30.2 late3 send30", "x3v": "send21 candR2", "b31.0": "flatT1",
    "b31.1": "load30", "a31.3": "store2", "a31.4": "fin3", "p31": "stateT1", "e31": "aheadT1 store3",
    "end0": "sum31.0 sum31.1 sum31.2 load21 send31 lookR2 candT1 lookT1 fin2", "end1": "shareR3",
    "end2": "fin0 stateT2 aheadT2", "end3": "candT2", "end4": "fin1", "end5": "load31 rowsR3 lookT2 shareT3 out0"}
PLAN = {name: place for place in PLACES for name in PLACES[place].split()}

SCRATCH = {
    "v1": ("sbuf", [128, 8192], "bfloat16"),
    "v2": ("sbuf", [128, 8192], "bfloat16"),
    "v3": ("sbuf", [128, 8192], "bfloat16"),
    "win": ("sbuf", [128, 4112], "bfloat16"),
    "ad": ("sbuf", [128, 768], "bfloat16"),
    "ab": ("sbuf", [128, 512], "int32"),
    "abu": ("sbuf", [128, 512], "uint16"),
    "abf": ("sbuf", [128, 512], "float32"),
    "xu": ("sbuf", [128, 4096], "bfloat16"),
    "abz": ("sbuf", [128, 256], "uint16"),
    "w1": ("sbuf", [128, 256], "int32"),
    "cdi": ("sbuf", [128, 256], "int32"),
    "cdu": ("sbuf", [128, 256], "uint16"),
    "cdf": ("sbuf", [128, 256], "float32"),
    "tpi": ("sbuf", [128, 128], "int32"),
    "lst": ("sbuf", [128, 512], "uint16"),
    "chl": ("sbuf", [128, 64], "bfloat16"),
    "tw": ("sbuf", [128, 2048], "bfloat16"),
    "ww": ("sbuf", [128, 864], "bfloat16"),
    "wp": ("sbuf", [128, 304], "bfloat16"),
    "bnd": ("sbuf", [128, 160], "bfloat16"),
    "sel": ("sbuf", [128, 16], "float32"),
    "eye": ("sbuf", [128, 128], "float32"),
    "tpf": ("sbuf", [128, 128], "float32"),
    "stt": ("sbuf", [128, 32], "float32"),
    "dd": ("sbuf", [128, 384], "float32"),
    "off": ("sbuf", [128, 192], "uint16"),
    "oa": ("sbuf", [128, 96], "uint16"),
    "sm": ("sbuf", [128, 128], "float32"),
    "gp": ("sbuf", [128, 256], "bfloat16"),
    "cnt": ("sbuf", [128, 768], "bfloat16"),
    "su": ("sbuf", [128, 16], "uint16"),
    "sb": ("sbuf", [128, 32], "bfloat16"),
    "ctab": ("dram", [2, 128, 32], "bfloat16"),
    "ln0": ("sbuf", [128, 128], "float32"),
    "ln1": ("sbuf", [128, 128], "float32"),
    "ln2": ("sbuf", [128, 128], "float32"),
    "lb3": ("dram", [8, 128, 32], "bfloat16"),
    "lb4": ("dram", [8, 128, 16], "float32"),
    "pp": ("psum", [128, 512], "float32"),
    "pl": ("psum", [128, 512], "float32"),
}
for _k in range(2):
    for _n in ("tb", "vc"):
        SCRATCH["%s%d" % (_n, _k)] = ("sbuf", [128, 2048], "bfloat16")
    SCRATCH["gq%d" % _k] = ("sbuf", [128, 512], "bfloat16")
for _n in ("px0", "px1", "pd0", "pd1", "pd2", "pv"):
    SCRATCH[_n] = ("psum", [128, 512], "float32")
for _k in range(6):
    SCRATCH["la%d" % _k] = ("dram", [8, 128, 16], "bfloat16")
    SCRATCH["sg%d" % _k] = ("dram", [8, 128, 16], "bfloat16")

SEMAPHORES = (["cv", "cs", "ct", "cg", "loc"] + ["aa%d" % k for k in range(6)] + ["ab%d" % k for k in range(5)]
              + ["d%d" % k for k in range(80)])
SIZE = {"bfloat16": 2, "uint16": 2, "float32": 4, "int32": 4}
A = AluOpType
F = ActivationFunctionType
WC, WF, WS, WE = 0, 144, 288, 720


def deal_engines(src, cores, topo, many):
    far = [c for c in cores if topo.chip(c) != topo.chip(src)]
    near = [c for c in cores if c != src and topo.chip(c) == topo.chip(src)]
    pool = topo.engines(src, far[0])
    k = 1
    while 2 * k * len(far) <= len(pool):
        k *= 2
    out = {c: pool[k * n:k * n + k] for n, c in enumerate(far)}
    used = pool[:k * len(far)]
    for c in near:
        out[c] = [e for e in topo.engines(src, c) if e not in used][:k]
        used = used + out[c]
    return {c: out[c] if many is True else out[c][many:many + 1] for c in out}


def rank_program(g, core, T, topo):
    r = T.rank_of(core)
    if r is None:
        return
    cores = list(T.cores)
    Q = {"g": g, "v": g.vector, "s": g.scalar, "t": g.tensor, "y": g.sync}
    V, S, PE = g.vector, g.scalar, g.tensor
    known = {q: {} for q in Q}
    total = {}
    recs = {}
    ndma = [0]

    def span(reg):
        name, c0, c1 = reg
        where, shape, dtp = SCRATCH[name.split(".")[0]]
        if where != "sbuf":
            return (name, 0, 1 << 30)
        z = SIZE[dtp]
        return (name, c0 * z // 16 * 16, (c1 * z + 15) // 16 * 16)

    def op(q, fn, reads, writes, dma=False, beside=()):
        rd = [span(x) for x in reads]
        wr = [span(x) for x in writes]
        needs = {}
        for writing, regs in ((False, rd), (True, wr)):
            for (n, a, b) in regs:
                ps = n in SCRATCH and SCRATCH[n][0] == "psum"
                for (q2, wrote, a2, b2, s2, v2, clock) in recs.get(n, []):
                    if ((q2 != q if ps else (wrote or writing) and a < b2 and a2 < b) and s2 not in beside
                            and needs.get(s2, (0, None))[0] < v2):
                        needs[s2] = (v2, clock)
        for s2 in needs:
            v2 = needs[s2][0]
            if known[q].get(s2, 0) >= v2:
                continue
            if any(s3 != s2 and needs[s3][1].get(s2, 0) >= v2 for s3 in needs):
                continue
            Q[q].wait_ge(T.sem[s2], v2)
        for s2 in needs:
            for s3, v3 in needs[s2][1].items():
                if known[q].get(s3, 0) < v3:
                    known[q][s3] = v3
        res = fn()
        if res is None:
            return
        if dma:
            sem = "d%d" % ndma[0]
            ndma[0] += 1
            val = 16 * len(res)
            for ins in res:
                ins.then_inc(T.sem[sem], 16)
        else:
            sem = "c" + q
            val = total.get(sem, 0) + 1
            res.then_inc(T.sem[sem], 1)
        total[sem] = val
        clock = dict(known[q])
        clock[sem] = val
        for wrote, regs in ((False, rd), (True, wr)):
            for (n, a, b) in regs:
                recs.setdefault(n, []).append((q, wrote, a, b, sem, val, clock))
        return sem

    def dma(q, pairs, reads, writes, beside=()):
        return op(q, lambda: [Q[q].dma_start(o, i) for (o, i) in pairs], reads, writes, True, beside)

    def send(source, src_of, dst, land, sem, many):
        plans = {c: deal_engines(c, cores, topo, many) for c in cores}
        def fn():
            trs = []
            for k, c in enumerate(cores):
                if c == core:
                    continue
                rid, pid, _ = topo.addr(c)
                trs.append(RemoteDMATransfer(dst_ids=[DstId(rid=rid, pnc=pid)],
                                             dma_engine_mask=sum(1 << e for e in plans[core][c]),
                                             remote_sem=T.sem[sem], src=src_of(k), dst=dst))
            g.remote_dma_fused(trs, local_sem=T.sem.loc)
            total["loc"] = total.get("loc", 0) + sum(len(plans[core][c]) for c in plans[core])
        op("g", fn, [source], [])
        total[sem] = sum(len(plans[c][core]) for c in cores if c != core)
        for reg in land:
            recs.setdefault(reg[0], []).append(("far", True) + span(reg)[1:] + (sem, total[sem], {sem: total[sem]}))

    def exchange(pairs, reg, source, src_of, land, sem, q, many=True):
        dma(q, pairs, [reg], [(land, 0, 1), source])
        send(source, src_of, T[land][r], [(land, 0, 1)], sem, many)

    def spread(src, reg, land, sem, staged):
        if staged:
            exchange([(T[land][r], src)], reg, (land, 0, 1), lambda k: T[land][r], land, sem, "y")
        else:
            dma("y", [(T[land][r], src)], [reg], [(land, 0, 1)])
            send(reg, lambda k: src, T[land][r], [(land, 0, 1)], sem, True)

    def vts(dst, d0, d1, src, s0, s1, *ops):
        a = (ops[1], None, ops[0]) if len(ops) == 2 else (ops[1], ops[3], ops[0], ops[2])
        op("v", lambda: V.tensor_scalar(T[dst][:, d0:d1], T[src][:, s0:s1], *a), [(src, s0, s1)], [(dst, d0, d1)])

    def vtt(dst, d0, n, a, a0, b, b0, o):
        op("v", lambda: V.tensor_tensor(T[dst][:, d0:d0 + n], T[a][:, a0:a0 + n], T[b][:, b0:b0 + n], o),
           [(a, a0, a0 + n), (b, b0, b0 + n)], [(dst, d0, d0 + n)])

    def vcp(dst, d0, src, s0, n, step=1):
        d1 = d0 + step * (n - 1) + 1
        op("v", lambda: V.tensor_copy(T[dst][:, d0:d1:step], T[src][:, s0:s0 + n]), [(src, s0, s0 + n)], [(dst, d0, d1)])

    def act(dst, d0, src, n, func):
        op("s", lambda: S.activation(T[dst][:, d0:d0 + n], T[src][:, 0:n], func), [(src, 0, n)], [(dst, d0, d0 + n)])

    def fill(dst, d0, d1, value):
        op("v", lambda: V.memset(T[dst][:, d0:d1], value), [], [(dst, d0, d1)])

    def gather(q, dst, d0, win, w0, w1, ofs, o0, o1, minus=None, other=None, how=A.min):
        n = 16 * (o1 - o0)
        if n <= 0:
            return
        src = T[win][:, w0:w1].indirect(T[ofs][:, o0:o1])
        out = T[dst][:, d0:d0 + n]
        reads = [(win, w0, w1)] + [(n, o0, o1) for n in (["off.0", "off.1"] if ofs == "off" else [ofs])]
        if other:
            reads.append((other[0], other[1], other[1] + n))
            fn = lambda: V.tensor_tensor(out, src, T[other[0]][:, other[1]:other[1] + n], how)
        elif minus is not None and q == "v":
            fn = lambda: V.tensor_scalar(out, src, -1.0, minus, A.mult, A.add)
        elif minus is not None:
            fn = lambda: S.activation(out, src, F.Identity, bias=minus, scale=-1.0)
        elif q == "v":
            fn = lambda: V.tensor_copy(out, src)
        else:
            fn = lambda: S.activation(out, src, F.Copy)
        op(q, fn, reads, [(dst, d0, d0 + n)])

    work = []

    def at(place):
        for name, fn in work:
            if PLAN[name] == place:
                fn()

    def by_list(q, j):
        dst, d0, win, w1 = (("v2", 2048, "v1", 8192), ("xu", 2048, "v2", 6144), ("v3", 2048, "v2", 8192),
                            ("xu", 2048, "v3", 6144))[j]
        c0, c1 = (0, SHARE[j]) if q == "s" else (SHARE[j], 128)
        gather(q, dst, d0 + 16 * c0, win, 2048, w1, "lst", 128 * j + c0, 128 * j + c1)
        at("x%d%s" % (j, q))

    def level(k, l, done):
        v, tb = "v%d" % k, "tb%d" % l
        w, w0, w1 = (v, 2048, 4096 + 2048 * l) if l == 0 or k == 1 else ("xu", 0, 4096)
        ofs, ob, oa = "abu", 256 * l, 256 * l + 128
        cuts = CUTS[2 * (k - 1) + l]
        last = len(cuts) - 1
        for n in range(last):
            c0, c1 = cuts[n], cuts[n + 1]
            h = 128 - HELP[2 * (k - 1) + l]
            gather("s", tb, 16 * c0, w, w0, w1, ofs, ob + c0, ob + min(h, c1), 255.0)
            if n == 0:
                gather("v", tb, 16 * h, w, w0, w1, ofs, ob + h, ob + 128, 255.0)
            at("b%d%d.%d" % (k, l, n))
            o = 4096 + 2048 * l
            gather("v", v, o + 16 * c0, w, w0, w1, ofs, oa + c0, oa + c1, None, (tb, 16 * c0))
            if c0 // 16 < c1 // 16:
                done(c0 // 16, c1 // 16)
            at("a%d%d.%d" % (k, l, n))

    def votes(k, l):
        v, vc = "v%d" % k, "vc%d" % l
        o = 4096 + 2048 * l
        parts = [[t for t in range(3) if 128 * t < 48 * u + 48 and 48 * u < 128 * t + 128] for u in range(8)]
        left = [2 * sum(t in p for p in parts) for t in range(3)]
        whole = list(left)
        def pack(src, s0, u0, u1):
            def fn():
                for u in range(u0, u1):
                    for t in parts[u]:
                        left[t] -= 1
                        c = 128 - 48 * u + 128 * t
                        ins = PE.matmul(T["pd%d" % t][:, 0:256], T.wp[:, c:c + 128], T[src][:, s0 + 256 * u:s0 + 256 * u + 256],
                                        left[t] + 1 == whole[t], left[t] == 0)
                return ins
            op("t", fn, [("wp", 0, 304), (src, s0 + 256 * u0, s0 + 256 * u1)],
               [("pd%d" % t, 0, 256) for t in range(parts[u0][0], parts[u1 - 1][-1] + 1)])
        def cands(q, u0, u1):
            gather(q, vc, 256 * u0, v, 2048, o + 256 * u1, "cdu", 128 * l + 16 * u0, 128 * l + 16 * u1, 0.0)
        def not_zero(t):
            if who[t] == "v":
                vts("ad", 256 * t, 256 * t + 256, "pd%d" % t, 0, 256, A.not_equal, 0.0)
            else:
                act("ad", 256 * t, "pd%d" % t, 256, F.Abs)
        def add(t):
            def fn():
                for m in range(2):
                    c = WS + 144 * t + 15 - m
                    ins = PE.matmul(T.pv[:, 0:128], T.ww[:, c:c + 128], T.ad[:, 256 * t + 128 * m:256 * t + 128 * m + 128],
                                    t + m == 0, t + m == 3)
                return ins
            op("t", fn, [("ww", WS, WS + 432), ("ad", 256 * t, 256 * t + 256)], [("pv", 0, 128)])
        (a, b, c), who = PACK[2 * (k - 1) + l]
        if not who:
            level(k, l, lambda u0, u1: None)
            return
        level(k, l, lambda u0, u1: pack(v, o, u0, u1))
        cands("s", 0, a)
        pack(vc, 0, 0, a)
        cands("s", a, b)
        at("p%d%d" % (k, l))
        cands("v", b, c)
        for u0, u1 in sorted([(a, b), (b, c)], key=lambda x: x[1] - x[0] + (a - 2 if x[0] == a else 0)):
            if u0 < u1:
                pack(vc, 0, u0, u1)
        at("c%d%d.0" % (k, l))
        cands("v", c, 8)
        pack(vc, 0, c, 8)
        work[0:3] = [("sum%d%d.%d" % (k, l, t), lambda t=t: [not_zero(t), add(t)]) for t in range(3)]
        at("e%d%d" % (k, l))

    def unequal(i0, i1):
        if i0 == i1:
            return
        gather("v", "vc1", 128 * i0, "v2", 2048, 8192, "cdu", 128 + 8 * i0, 128 + 8 * i1, None, ("tw", 128 * i0), A.not_equal)
        def fn():
            for i in range(i0, i1):
                ins = PE.matmul(T.px1[:, 0:128], T.ww[:, WE + 15 - i:WE + 143 - i], T.vc1[:, 128 * i:128 * i + 128],
                                i == 0, i == 15)
            return ins
        op("t", fn, [("ww", WE, WE + 144), ("vc1", 128 * i0, 128 * i1)], [("px1", 0, 128)])

    def send_votes(k, l, q, dq):
        ph = 2 * (k - 1) + l
        la, sg = "la%d" % ph, "sg%d" % ph
        c0 = 128 * ph
        pv = "px1" if ph == 3 else "pv"
        if q == "v":
            vcp("cnt", c0, pv, 0, 128)
        else:
            act("cnt", c0, pv, 128, F.Copy)
        exchange([(T[sg][:], T.cnt[:, c0:c0 + 128]), (T[la][r], T.cnt[16 * r:16 * r + 16, c0:c0 + 128])],
                 ("cnt", c0, c0 + 128), (sg, 0, 1), lambda j: T[sg][j], la, "aa%d" % ph, dq, ph if ph < 2 else True)

    def window(k):
        return ("v1", 2048) if k == 3 else ("win", 0)

    def load_counts(k, l, qs="y"):
        la = "la%d" % (2 * (k - 1) + l)
        w, b = window(k)
        c0 = b + 16 + 2048 * l
        mine = []
        for n, q in enumerate(qs):
            mine.append(dma(q, [(T[w][16 * j:16 * j + 8, c0:c0 + 2048], T[la][:]) for j in range(n, 8, len(qs))],
                            [(la, 0, 1)], [(w, c0, c0 + 2048)], mine))

    def load_cands(k):
        w, b = window(k)
        dma("y", [(T[w][16 * j + 8:16 * j + 10, b + 16:b + 4112], T.ctab[:]) for j in range(8)],
            [("ctab", 0, 1)], [(w, b + 16, b + 4112)])

    def pick(ps, p0, wt, src, s0, s1, step=1):
        n = ((s1 - s0) // 16 - 1) * step + 1
        def fn():
            for i in range(16):
                c = wt + 15 - i
                ins = PE.matmul(T[ps][:, p0:p0 + n:step], T.ww[:, c:c + 128], T[src][:, s0 + i:s1:16], i == 0, i == 15)
            return ins
        op("t", fn, [("ww", wt, wt + 144), (src, s0, s1)], [(ps, p0, p0 + n)])

    def track(slot, lane, src, reg):
        d, o = 64 * slot + 3 * lane, 32 * slot + lane
        for out, where in ([(T.off[:, o:o + 31:2], ("off.%d" % lane, 32 * slot, 32 * slot + 32))]
                           + [(T.oa[:, 16 * slot:16 * slot + 16], ("oa", 16 * slot, 16 * slot + 16))] * lane):
            op("v", lambda: V.tensor_scalar(out, src, 2032.0, 15.0, A.subtract, A.max), [reg], [where])
        op("v", lambda: V.tensor_copy(T.dd[:, d:d + 61:4], src), [reg], [("dd.%d" % lane, 64 * slot, 64 * slot + 64)])

    def look(qs, slot, k, l):
        w, b = window(k)
        per = 32 // len(qs)
        for n, q in enumerate(qs):
            o = 32 * slot + per * n
            gather(q, "gq%d" % l, 16 * per * n, w, b, b + 16 + 2048 * (l + 1), "off", o, o + per)
        pick("px%d" % l, 257, WC, "gq%d" % l, 0, 512, 2)

    def choose(slot, l):
        px, c, s = "px%d" % l, 64 * slot, 64 * l
        op("v", lambda: V.tensor_tensor_scan(T.sm[:, s:s + 64], T[px][:, 256:320], T.dd[:, c:c + 64], 0.0, A.subtract, A.min),
           [(px, 0, 1), ("dd.0", c, c + 64), ("dd.1", c, c + 64), ("dd.3", 0, 384)], [("sm", s, s + 64)])
        return T.sm[:, s + 3:s + 64:4], ("sm", s, s + 64)

    def share_list(slot, l, j, nxt=None):
        ln, c = "ln%d" % j, 16 * r
        new, reg = choose(slot, l)
        op("v", lambda: V.tensor_copy(T[ln][:, c:c + 16], new), [reg], [(ln, c, c + 16)])
        send((ln, c, c + 16), lambda k: T[ln][:, c:c + 16], T[ln][:, c:c + 16], [(ln, 0, c), (ln, c + 16, 128)],
             "ab%d" % j, True)
        if nxt:
            track(nxt, 1, new, reg)

    def load_list(j):
        ln = "ln%d" % j
        op("t", lambda: PE.matmul(T.pl[:, 0:128], T[ln][:, 0:128], T.eye[:, 0:128], True, True),
           [(ln, 0, 128), ("eye", 0, 128)], [("pl", 0, 128)])
        vcp("lst", 128 * (j + 1), "pl", 0, 128)

    def ahead_gather(slot, w, b, l):
        gather("s", "gp", 0, w, b, b + 16 + 2048 * (l + 1), "oa", 16 * slot, 16 * slot + 16)
        pick("pp", 0, WF, "gp", 0, 256)

    def ahead_finish(slot):
        track(slot, 0, T.pp[:, 0:16], ("pp", 0, 16))

    def store_values(c0, c1, q="s"):
        dma(q, [(T.yv[:, c0:c1], T.v3[:, 2048 + c0:2048 + c1])], [("v3", 2048 + c0, 2048 + c1)], [])

    def count_up(name, c0, n, step, base, cm):
        kw = {} if SCRATCH[name][2] == "int32" else {"allow_small_or_imprecise_dtypes": True}
        op("g", lambda: g.iota(T[name][:, c0:c0 + n], [[step, n]], base, cm, **kw), [], [(name, c0, c0 + n)])

    def keep(name, c0, s0, n, pattern, cmp, other, base, cm):
        op("g", lambda: g.affine_select(T[name][:, c0:c0 + n], T[name][:, s0:s0 + n], pattern, cmp, other, base, cm),
           [(name, s0, s0 + n)], [(name, c0, c0 + n)])

    def band(c, s, lo, hi):
        op("g", lambda: g.affine_select(T.bnd[:, 8:16], T.bnd[:, s:s + 8], [[-16, 8]], A.is_ge, 0.0, -lo, 1),
           [("bnd", s, s + 8)], [("bnd", 8, 16)])
        op("g", lambda: g.affine_select(T.ww[:, c:c + 113:16], T.bnd[:, 8:16], [[16, 8]], A.is_ge, 0.0, hi, -1),
           [("bnd", 8, 16)], [("ww", c, c + 113)])

    R0, T0, R1, T1, R2, T2 = range(6)

    dma("y", [(T.ab[:, 0:128], T.fb[:, 0:128])], [], [("ab", 0, 128)])
    dma("s", [(T.ab[:, 128:256], T.fa[:, 0:128])], [], [("ab", 128, 256)])
    dma("s", [(T.v1[:, 2048:4096], T.x[:])], [], [("v1", 2048, 4096)])
    dma("y", [(T.cdi[:], T.cd[:])], [("ab", 0, 256)], [("cdi", 0, 256)])
    dma("y", [(T.ab[:, 256:384], T.fb[:, 128:256]), (T.ab[:, 384:512], T.fa[:, 128:256])], [("v1", 2048, 4096)],
        [("ab", 256, 512)])
    dma("y", [(T.tpi[:], T.tp[:])], [], [("tpi", 0, 128)])
    count_up("w1", 0, 16, 0, 0, 1)
    count_up("stt", 0, 16, 1, 2048, 16)
    fill("wp", 0, 304, 0.0)
    fill("ww", 0, 864, 0.0)
    op("v", lambda: V.memset(T.dd[:, 1:384:4], 0.0), [], [("dd.2", 0, 384)])
    op("v", lambda: V.memset(T.dd[:, 2:384:4], BIG), [], [("dd.3", 0, 384)])
    for px in ("px0", "px1"):
        op("v", lambda: V.memset(T[px][:, 256:320:4], 2 * BIG), [], [(px, 0, 1)])
        op("v", lambda: V.memset(T[px][:, 258:320:4], 0.0), [], [(px, 0, 1)])
    vts("w1", 16, 32, "w1", 0, 16, A.bitwise_and, 8)
    track(R0, 1, T.stt[:, 0:16], ("stt", 0, 16))
    vts("win", 0, 16, "w1", 16, 32, A.is_equal, 0.0)
    fill("win", 16, 2064, 0.0)
    vcp("abu", 0, "ab", 0, 256)
    fill("win", 2064, 4112, 0.0)
    count_up("wp", 128, 48, 0, 65536, 0)
    keep("wp", 128, 128, 48, [[-16, 8], [-3, 6]], A.is_ge, 256.0, -2, 1)
    keep("wp", 128, 128, 48, [[-16, 8], [-3, 6]], A.is_ge, 1.0, -1, 1)
    keep("wp", 128, 128, 48, [[-16, 8], [-3, 6]], A.is_ge, 0.0, 0, 1)
    keep("wp", 128, 128, 48, [[16, 8], [3, 6]], A.is_ge, 0.0, 2, -1)
    keep("wp", 128, 128, 48, [[16, 8], [0, 6]], A.is_ge, 0.0, 15, -1)
    count_up("bnd", 32, 64, 0, 1, 0)
    for t in range(3):
        c = WS + 144 * t + 15
        keep("bnd", 96, 32, 64, [[-6, 8], [-48, 8]], A.is_ge, 0.0, 128 * t, 1)
        op("g", lambda: g.affine_select(T.ww[:, c:c + 127:2], T.bnd[:, 96:160], [[6, 8], [48, 8]], A.is_ge, 0.0,
                                        5 - 128 * t, -1), [("bnd", 96, 160)], [("ww", c, c + 127)])
    count_up("sel", 0, 16, 0, 1, 0)
    keep("sel", 0, 0, 16, [[-1, 16]], A.is_equal, 0.0, -16 * r, 1)
    band(WF + 15, 32, 8, 9)
    band(WE + 15, 32, 0, 15)
    count_up("bnd", 0, 8, 0, BIG, 0)
    keep("bnd", 0, 0, 8, [[16, 8]], A.is_ge, 1.0, 7, -1)
    band(WC + 15, 0, 0, 9)
    count_up("eye", 0, 128, 0, 1, 0)
    keep("eye", 0, 0, 128, [[-1, 128]], A.is_equal, 0.0, 0, 1)

    def turn():
        PE.matmul(T.pp[:, 0:16], T.cdf[:, 0:256:2], T.sel[:, 0:16], True, True)
        return PE.matmul(T.pp[:, 16:32], T.cdf[:, 1:256:2], T.sel[:, 0:16], True, True)
    def split():
        vcp("chl", 0, "pp", 0, 32)
        vtt("chl", 32, 32, "pp", 0, "chl", 0, A.subtract)
        dma("y", [(T.ctab[0], T.chl[:, 0:32]), (T.ctab[1], T.chl[:, 32:64])], [("chl", 0, 64)], [("ctab", 0, 1)])
    def turn_lists():
        PE.matmul(T.pl[:, 0:16], T.cdf[:, 0:128], T.sel[:, 0:16], True, True)
        return PE.matmul(T.pl[:, 16:32], T.tpf[:, 0:128], T.sel[:, 0:16], True, True)
    def first_states():
        track(R0, 0, T.pl[:, 0:16], ("pl", 0, 16))
        track(T0, 1, T.pl[:, 16:32], ("pl", 0, 16))
    def last_list(ps, out, c):
        vtt("abf", 256 + c, 128, ps, 0, "abf", 256 + c, A.min)
        dma("y" if c == 0 else "s", [(out[:, 128:256], T.abf[:, 256 + c:384 + c])], [("abf", 256 + c, 384 + c)], [])
    def share_last():
        new, reg = choose(R2, 0)
        op("v", lambda: V.tensor_copy(T.sb[:, 0:32:2], new), [reg], [("sb", 0, 32)])
        op("v", lambda: V.tensor_tensor(T.sb[:, 1:32:2], new, T.sb[:, 0:32:2], A.subtract),
           [reg, ("sb", 0, 32)], [("sb", 0, 32)])
        spread(T.sb[:, 0:32], ("sb", 0, 32), "lb3", "ab3", STAGE[0])
    def share_taps():
        new, reg = choose(T2, 1)
        op("v", lambda: V.tensor_copy(T.stt[:, 16:32], new), [reg], [("stt", 16, 32)])
        spread(T.stt[:, 16:32], ("stt", 16, 32), "lb4", "ab4", STAGE[1])
    def inputs_again(k, q):
        dma(q, [(T.xu[:, 0:2048], T["v%d" % k][:, 2048:4096])], [("v%d" % k, 2048, 4096)], [("xu", 0, 2048)])

    cut = 4096 + 16 * CUTS[5][2]
    steps = [
        ("cand0", lambda: vcp("cdu", 0, "cdi", 0, 128)),
        ("fanb1", lambda: vcp("abu", 256, "ab", 256, 128)),
        ("candf", lambda: vcp("cdf", 0, "cdi", 0, 256)),
        ("send10", lambda: send_votes(1, 0, LQ[4], DQ[0])),
        ("turn", lambda: op("t", turn, [("cdf", 0, 256), ("sel", 0, 16)], [("pp", 0, 32)])),
        ("fana1", lambda: vcp("abu", 384, "ab", 384, 128)),
        ("table", lambda: [split(), load_cands(1)]),
        ("tapf", lambda: [vcp("tpf", 0, "tpi", 0, 128),
                          op("t", turn_lists, [("cdf", 0, 128), ("tpf", 0, 128), ("sel", 0, 16)], [("pl", 0, 32)])]),
        ("cand1", lambda: vcp("cdu", 128, "cdi", 128, 128)),
        ("first", first_states),
        ("taps0", lambda: vcp("lst", 0, "tpi", 0, 128)),
        ("load10", lambda: load_counts(1, 0)),
        ("send11", lambda: send_votes(1, 1, LQ[5], DQ[1])),
        ("table3", lambda: [vcp("v1", 2048, "win", 0, 16), load_cands(3)]),
        ("lookR0", lambda: look(LQ[0], R0, 1, 0)),
        ("shareR1", lambda: share_list(R0, 0, 0, R1)),
        ("load11", lambda: load_counts(1, 1)),
        ("aheadT0", lambda: ahead_gather(T0, "v1", 2048, 1)),
        ("candT0", lambda: ahead_finish(T0)),
        ("again2", lambda: inputs_again(2, DQ[9])),
        ("send20", lambda: send_votes(2, 0, LQ[6], DQ[2])),
        ("listR1", lambda: load_list(0)),
        ("aheadR1", lambda: ahead_gather(R1, "v1", 2048, 0)),
        ("lookT0", lambda: look(LQ[1], T0, 1, 1)),
        ("candR1", lambda: ahead_finish(R1)),
        ("shareT1", lambda: share_list(T0, 1, 1)),
        ("load20", lambda: load_counts(2, 0)),
        ("lookR1", lambda: look(LQ[7], R1, 2, 0)),
        ("listT1", lambda: load_list(1)),
        ("shareR2", lambda: share_list(R1, 0, 2, R2)),
        ("store0", lambda: store_values(0, 2048)),
        ("flatT1", lambda: dma("y", [(T.su[:, 0:16], T.lst[16 * r:16 * r + 16, 256:384])], [("lst", 256, 384)],
                               [("su", 0, 16)])),
        ("again3", lambda: inputs_again(3, DQ[10])),
        ("twin", lambda: dma("y", [(T.tw[:], T.v2[:, 6144:8192])], [("v2", 6144, 8192)], [("tw", 0, 2048)])),
        ("late0", lambda: unequal(0, LATE[0])),
        ("late1", lambda: unequal(LATE[0], LATE[1])),
        ("late2", lambda: unequal(LATE[1], LATE[2])),
        ("late3", lambda: unequal(LATE[2], 16)),
        ("send21", lambda: send_votes(2, 1, LQ[2], DQ[3])),
        ("aheadR2", lambda: ahead_gather(R2, "v1", 2048, 0)),
        ("listR2", lambda: load_list(2)),
        ("store1", lambda: store_values(2048, 4096)),
        ("candR2", lambda: ahead_finish(R2)),
        ("send30", lambda: send_votes(3, 0, LQ[8], DQ[4])),
        ("load21", lambda: load_counts(2, 1)),
        ("load30", lambda: load_counts(3, 0)),
        ("store2", lambda: store_values(4096, cut)),
        ("send31", lambda: send_votes(3, 1, LQ[3], DQ[5])),
        ("lookR2", lambda: look(LQ[9], R2, 3, 0)),
        ("stateT1", lambda: track(T1, 1, T.su[:, 0:16], ("su", 0, 16))),
        ("aheadT1", lambda: ahead_gather(T1, "win", 0, 1)),
        ("shareR3", share_last),
        ("fin0", lambda: vts("w1", 0, 256, "ab", 256, 512, A.subtract, 2040.0, A.max, 0.0)),
        ("candT1", lambda: ahead_finish(T1)),
        ("lookT1", lambda: look(LQ[10], T1, 2, 1)),
        ("store3", lambda: store_values(cut, 6144, DQ[6])),
        ("fin1", lambda: [vts("abz", 0, 256, "w1", 0, 256, A.mult, 2.0), fill("v2", 2032, 2048, BIG / 2)]),
        ("stateT2", lambda: track(T2, 1, *choose(T1, 1))),
        ("aheadT2", lambda: ahead_gather(T2, "win", 0, 1)),
        ("load31", lambda: load_counts(3, 1, DQ[7])),
        ("fin2", lambda: vcp("abf", 0, "ab", 0, 256)),
        ("candT2", lambda: ahead_finish(T2)),
        ("rowsR3", lambda: dma(DQ[8], [(T.v2[8:128:16, 2048:6144], T.lb3[:]), (T.v2[9:128:16, 2047:6143], T.lb3[:])],
                               [("lb3", 0, 1)], [("v2", 2047, 6144)])),
        ("lookT2", lambda: look("vs", T2, 3, 1)),
        ("fin3", lambda: vcp("abf", 256, "ab", 256, 256)),
        ("shareT3", share_taps),
        ("out0", lambda: dma("y", [(T.yb[:, 0:128], T.abf[:, 0:128]), (T.ya[:, 0:128], T.abf[:, 128:256])],
                             [("abf", 0, 256)], [])),
    ]
    work.extend(steps[0:3] + steps)
    work[0:3] = [("sum10.0", None)] * 3

    for k in (1, 2, 3):
        for l in (0, 1):
            if k > 1:
                by_list("s", 2 * (k - 2) + l)
                by_list("v", 2 * (k - 2) + l)
            votes(k, l)
    for n in range(8):
        at("end%d" % n)
    for tb, ps, c in (("tb1", "pd0", 0), ("tb0", "pd1", 128)):
        for h in (0, 64):
            gather("s", tb, 16 * h, "v2", 2032, 6144, "abz", c + h, c + h + 32)
            gather("v", tb, 16 * h + 512, "v2", 2032, 6144, "abz", c + h + 32, c + h + 64)
            pick(ps, h, WF, tb, 16 * h, 16 * h + 1024)
            at("f%d" % ((c + h) // 64))
            if c and not h:
                last_list("pd0", T.yb, 0)
    last_list("pd1", T.ya, 128)
    dma("y", [(T.yt[:], T.lb4[:])], [("lb4", 0, 1)], [])
    for s in total:
        if known["g"].get(s, 0) < total[s]:
            g.wait_ge(T.sem[s], total[s])
